import numpy as np, ml_dtypes
CORES = [24,25,26,27,28,29,30,31]
N = 8
BF = ml_dtypes.bfloat16
def gentries(a):
    return np.ascontiguousarray(a.reshape(8, 16, -1).transpose(0, 2, 1)).reshape(8, -1)
def gtable(e):
    e = np.asarray(e); return np.ascontiguousarray(e.reshape(8, -1, 16).transpose(0, 2, 1)).reshape(128, -1).astype(np.int32)
W, L, B, VI, PS, ST = 4096, 32, 128, 3, 3, 32
KAP = 113 * np.arange(L) + 37
def tables_of(rng):
    lv = rng.random((N, 8, 16, W), dtype=np.float32); x = rng.integers(0, 16, (N, 8, 16, W))
    h = rng.choice(np.array([0.15, 0.22, 0.3]), (N, 8, 1, 1)); w = rng.choice(np.array([0.12, 0.18]), (N, 8, 1, 1))
    e = np.where(lv < h, 12 + (x & 3), np.where(lv < h + w, x & 3, 4 + (x & 7)))
    nd = rng.choice(np.array([0.0, 0.05, 0.1, 0.2]), (N, 8, 1, W)); x = rng.integers(0, 12, (N, 8, 16, W))
    return e, np.where(rng.random((N, 8, 16, W), dtype=np.float32) < nd, 12 + (x & 3), x)
def own_steps(rng, s):
    return np.take_along_axis(s, rng.integers(0, L, (N, 8, L, B)), axis=2)
def pack(e, p, s, q, st, th):
    return {"eff": e.reshape(N, 128, W).astype(np.float32).astype(BF), "req": p.reshape(N, 128, W).astype(np.float32).astype(BF),
            "act": np.stack([gtable(a.reshape(8, L * B)) for a in s]), "why": np.stack([gtable(a.reshape(8, L * B)) for a in q]),
            "st0": np.ascontiguousarray(st).reshape(N, 128, B).astype(np.float32).astype(BF), "bar": np.stack([gtable(a) for a in th])}
def setup_inputs(rng):
    e, p = tables_of(rng); s = rng.integers(0, W, (N, 8, L, B)); w = rng.integers(0, 5, (N, 8, L, B))
    q = np.where(w < 2, -1, np.where(w < 4, own_steps(rng, s), rng.integers(0, W, (N, 8, L, B))))
    return pack(e, p, s, q, rng.integers(0, 16, (N, 8, 16, B)), rng.choice(np.array([0, 1, 2, 2, 3, 3, 4]), (N, 8, B)))
def setup_inputs_alike(rng):
    e, p = tables_of(rng)
    fw = np.concatenate([np.argsort(rng.random((N, 8, W - 2)), axis=-1)[..., :4] + 1, np.zeros((N, 8, 1), np.int64), np.full((N, 8, 1), W - 1)], axis=2)
    ix = np.broadcast_to(fw[:, :, None, :], (N, 8, 16, 6))
    np.put_along_axis(e, ix, rng.choice(np.array([0, 3, 4, 8, 11, 12, 15]), (N, 8, 16, 6)), axis=3)
    np.put_along_axis(p, ix, np.where(rng.random((N, 8, 16, 6)) < 0.2, 12, 11), axis=3)
    n = rng.integers(0, 6, (N, 8, L, B)); n[:, 1::2] = n[:, 1::2, :, :1]
    n = np.where(rng.random((N, 8, 1, B)) < 0.15, n[:, :, :1], n)
    s = np.take_along_axis(fw, n.reshape(N, 8, L * B), axis=2).reshape(N, 8, L, B)
    q = np.take_along_axis(fw, rng.integers(0, 6, (N, 8, L * B)), axis=2).reshape(N, 8, L, B)
    q = np.where(rng.random((N, 8, L, B)) < 0.4, -1, q)
    return pack(e, p, s, q, rng.integers(0, 16, (N, 8, 16, B)), rng.integers(0, 5, (N, 8, B)))
def setup_inputs_corners(rng):
    o = np.argsort(rng.random((N, 8, W)), axis=-1); kc = np.zeros((N, 8, W), np.int64)
    np.put_along_axis(kc, o, np.broadcast_to(np.arange(W) & 7, (N, 8, W)), axis=2)
    k4 = kc[:, :, None, :]; bit = rng.integers(0, 2, (N, 8, 16, W)) == 1
    e = np.where(bit, np.array([4, 0, 12, 4, 4, 4, 4, 4])[k4], np.array([11, 3, 15, 11, 11, 11, 11, 11])[k4])
    e = np.where(k4 == 7, np.array([3, 4, 11, 12])[rng.integers(0, 4, (N, 8, 16, W))], e)
    rk = ((2 * rng.integers(0, 8, (N, 8, 1, W)) + 1) * np.arange(16)[None, None, :, None] + rng.integers(0, 16, (N, 8, 1, W))) & 15
    nd = np.where(k4 == 7, rng.integers(0, 4, (N, 8, 1, W)), np.array([0, 0, 0, 1, 2, 3, 16, 0])[k4]); bit = rng.integers(0, 2, (N, 8, 16, W)) == 1
    p = np.where(rk < nd, np.where(bit, 12, 15), np.where(bit, 11, 0))
    tp = rng.integers(0, 8, (N, 8, 1, B)); y = rng.integers(4, 7, (N, 8, 1, B)); v = rng.integers(1, L, (N, 8, 1, B)); kk = np.arange(L)[None, None, :, None]
    j = rng.choice(np.array([0, L // 2, L - 2]), (N, 8, 1, B)); cp = np.zeros((N, 8, L, B), np.int64)
    cp = np.where((tp == 1) & (kk == 0), y, cp)
    cp = np.where((tp == 2) & (kk == j), 1, cp); cp = np.where((tp == 2) & (kk == L - 1), y, cp)
    cp = np.where(tp == 3, 3, cp)
    for a, b in ((L // 3, 4), (L // 2, 5), (L - 1, 6)): cp = np.where((tp == 4) & (kk == a), b, cp)
    cp = np.where(tp == 5, np.where(kk == v, y, 1), cp)
    cp = np.where((tp == 6) & (kk == 0), 2, cp); cp = np.where((tp == 6) & (kk == L - 1), 1, cp)
    cp = np.where(tp == 7, rng.integers(0, 8, (N, 8, L, B)), cp)
    s = np.take_along_axis(o, (8 * rng.integers(0, W // 8, (N, 8, L, B)) + cp).reshape(N, 8, L * B), axis=2).reshape(N, 8, L, B)
    st = np.array([7, 8, 0, 15])[rng.integers(0, 4, (N, 8, 16, B))]
    st = np.where((tp == 1) | (tp == 3) | (tp == 4), 7, np.where(tp == 2, 8, st))
    h = np.where(tp == 2, j, np.where(tp == 5, v - 1, np.where(tp == 4, L // 3, 0))); own = np.take_along_axis(s, h, axis=2)
    qm = rng.integers(0, 4, (N, 8, 1, B))
    q = np.where(qm == 0, -1, np.where(qm == 1, own, np.where(qm == 2, np.where(rng.random((N, 8, L, B)) < 0.5, own, -1), own_steps(rng, s))))
    return pack(e, p, s, q, st, rng.choice(np.array([0, 1, 2, 3, 16]), (N, 8, B)))
def setup_inputs_ends(rng):
    t = W - 1
    e = 15 * (rng.random((N, 8, 16, W), dtype=np.float32) < rng.choice(np.array([0.0, 0.1, 0.5, 0.9, 1.0]), (N, 8, 1, W))).astype(np.int64)
    p = 15 * (rng.random((N, 8, 16, W), dtype=np.float32) < rng.choice(np.array([0.0, 0.0, 0.1, 0.3, 1.0]), (N, 8, 1, W))).astype(np.int64)
    kk = np.arange(L)[None, None, :, None]; x = rng.choice(np.array([0, 1, L // 2, L - 2, L - 1, L]), (N, 8, 1, B)); x[..., B - 1] = L - 2; x[..., B - 2] = L - 1
    m = rng.random((N, 8, 1, B)) < 0.6; m[..., B - 2:] = True
    s = t * np.where(m, (kk >= x).astype(np.int64), rng.integers(0, 2, (N, 8, L, B)))
    q = np.where(rng.random((N, 8, L, B)) < rng.choice(np.array([0.0, 0.2, 0.5, 1.0]), (N, 8, 1, B)), t, -1)
    st = 15 * (rng.random((N, 8, 16, B)) < rng.choice(np.array([0.0, 0.5, 1.0]), (N, 8, 1, B))).astype(np.int64)
    th = 16 * rng.integers(0, 2, (N, 8, B)); th[..., B - 1] = 16; th[..., B - 2] = 0
    c0 = (KAP * t) & t; c1 = ((t * t >> 5) + KAP * t) & t
    for r in range(N):
        for g in range(8):
            k = (N + 7 - r - g) & 3; u = e[r, g]
            if k == 3: continue
            if k == 0:
                u[0, c0] = 0; u[:, c0[L - 1]] = 15; u[:, 0] = 0; u[:, t] = 15 * rng.integers(0, 2, 16)
            elif k == 1:
                u[:, c1[[1, 2, L - 1]]] = 15; u[5, c1[0]] = 0; u[:, 0] = 15; u[:, t] = 0
            else:
                u[:, c1] = 0; u[:, 0] = 15; u[:, t] = 15; u[rng.permutation(16)[:2], t] = 0
            p[r, g, :, 0] = 0; p[r, g, :, t] = 15
    return pack(e, p, s, q, st, th)
def setup_inputs_full(rng):
    e, p = tables_of(rng); s = rng.integers(0, W, (N, 8, L, B)); st = rng.integers(0, 16, (N, 8, 16, B)); th = rng.choice(np.array([0, 1, 2, 2, 3, 3, 4]), (N, 8, B)); kk = np.arange(L)[:, None]
    for r in range(N):
        for g in range(8):
            m = (g + r + 2 - N) & 7
            if m > 4: continue
            o = rng.permutation(W).reshape(32, W // 32); kc = np.zeros(W, np.int64); kc[o] = np.arange(32)[:, None]
            y = rng.integers(0, 4, (16, W)); e[r, g] = np.where(kc < 17, rng.integers(4, 12, (16, W)), np.where(kc < 20, y, 12 + y))
            rk = ((2 * rng.integers(0, 8, W) + 1) * np.arange(16)[:, None] + rng.integers(0, 16, W)) & 15
            p[r, g] = np.where((rk < kc) & (kc < 17), rng.integers(12, 16, (16, W)), rng.integers(0, 12, (16, W)))
            n = rng.integers(2, 16, B) if m == 0 else rng.integers(4, 17, B)
            x = rng.choice(np.array([0, L // 2, L - 1, L - 1]), B); j = rng.integers(0, L, B); low = (j < x) & (rng.random(B) < 0.5)
            calm = rng.random(B) < (0.1 if m else 0.0)
            if m: calm[B // 2] = True
            kd = np.where(kk == x, n, np.where(kk > x, rng.integers(0, 32, (L, B)), 0)); kd = np.where((kk == j) & low, rng.integers(17, 20, B), kd); kd = np.where(calm, 0, kd)
            s[r, g] = o[kd, rng.integers(0, W // 32, (L, B))]
            st[r, g] = rng.integers(0, 8, (16, B)) + 8 * (low | calm).astype(np.int64)
            up = np.ones(B, np.int64) if m == 0 else rng.integers(0, 2, B)
            th[r, g] = np.minimum(n + up, 16)
    w = rng.integers(0, 5, (N, 8, L, B))
    q = np.where(w < 2, -1, np.where(w < 4, own_steps(rng, s), rng.integers(0, W, (N, 8, L, B))))
    return pack(e, p, s, q, st, th)
def setup_inputs_spread(rng):
    def power(hi, pw, shape): return np.minimum((hi * rng.random(shape, dtype=np.float32) ** pw.astype(np.float32)).astype(np.int64), hi - 1)
    e = power(16, rng.choice(np.array([0.5, 1.0, 2.0]), (N, 8, 16, 1)), (N, 8, 16, W))
    p = power(16, rng.choice(np.array([1.0, 3.0, 8.0, 20.0, 20.0]), (N, 8, 1, W)), (N, 8, 16, W))
    s = power(W, rng.choice(np.array([0.25, 1.0, 4.0]), (N, 8, L, 1)), (N, 8, L, B))
    q = np.where(rng.random((N, 8, L, B)) < 0.5, own_steps(rng, s), rng.integers(-1, W, (N, 8, L, B)))
    return pack(e, p, s, q, power(16, rng.choice(np.array([0.3, 1.0, 3.0]), (N, 8, 1, B)), (N, 8, 16, B)), power(17, rng.choice(np.array([1.0, 3.0, 6.0]), (N, 8, 1)), (N, 8, B)))
def check_inputs(d):
    bad = []
    for k, lo, hi in (("eff", 0, 15), ("req", 0, 15), ("act", 0, W - 1), ("why", -1, W - 1), ("st0", 0, 15), ("bar", 0, 16)):
        v = np.asarray(d[k]).astype(np.float64)
        if not (np.min(v) >= lo and np.max(v) <= hi): bad.append("range of " + k)
        elif np.any(v != np.floor(v)): bad.append("whole numbers in " + k)
    return bad
def pick(tab, ix):
    return np.stack([tab[g][:, ix[g]] for g in range(8)])
def visit(E, P, S, Q, s, th, R, t):
    kk = np.arange(L)[None, :, None]
    es = pick(E, S.reshape(8, L * B)).reshape(8, 16, L, B); ps = pick(P, S.reshape(8, L * B)).reshape(8, 16, L, B)
    flaw = np.zeros((8, 16, L, B), bool)
    for k in range(L):
        flaw[:, :, k] = (ps[:, :, k] >= 12) & (s < 8)
        s = np.where((es[:, :, k] >= 12) | (es[:, :, k] <= 3), es[:, :, k], s)
    over = np.add.reduce(flaw.astype(np.int16), axis=1) >= 2 + (R & 1)
    found = np.any(over, axis=1); ks = np.argmax(over, axis=1)
    fl = np.take_along_axis(flaw, ks[:, None, None, :], 2); need = np.take_along_axis(ps, ks[:, None, None, :], 2) >= 12
    low = np.any((es <= 3) & fl, axis=1) & (kk < ks[:, None, :])
    d = np.where(np.any(low, axis=1), L - 1 - np.argmax(low[:, ::-1], axis=1), ks)
    a = np.take_along_axis(S, ks[:, None, :], 1); z = np.take_along_axis(S, d[:, None, :], 1)
    c = ((a * z >> 5) + KAP[None, :, None] * a + 97 * t) & (W - 1)
    ec = pick(E, c.reshape(8, L * B)).reshape(8, 16, L, B)
    score = np.add.reduce(((ec >= 12) & fl).astype(np.int64), axis=1) - np.add.reduce(((ec <= 3) & need & ~fl).astype(np.int64), axis=1)
    m = np.argmax(score, axis=1); best = np.max(score, axis=1); cm = np.take_along_axis(c, m[:, None, :], 1)
    put = (found & (best >= th))[:, None, :]; ret = (found & (best < th))[:, None, :]
    kb = ks[:, None, :]
    si = np.where(kk < kb, S, np.where(kk == kb, cm, np.concatenate([S[:, :1], S[:, :-1]], axis=1)))
    qi = np.where(kk < kb, Q, np.where(kk == kb, z, np.concatenate([Q[:, :1], Q[:, :-1]], axis=1)))
    go = (kk == d[:, None, :]) | (Q == z)
    order = np.argsort(go, axis=1, kind="stable"); kept = kk < L - np.add.reduce(go.astype(np.int64), axis=1)[:, None, :]
    sr = np.where(kept, np.take_along_axis(S, order, 1), c); qr = np.where(kept, np.take_along_axis(Q, order, 1), -1)
    at = ST * np.arange(B)[None, :] + (np.add.reduce(s.astype(np.int64), axis=1) & (ST - 1))
    e2 = np.array(E); np.put_along_axis(e2, np.broadcast_to(at[:, None, :], (8, 16, B)), (pick(E, at) + s) >> 1, axis=2)
    return np.where(put, si, np.where(ret, sr, S)), np.where(put, qi, np.where(ret, qr, Q)), s, e2, int(np.count_nonzero(ret))
def reference(eff, req, act, why, st0, bar):
    E = [x.astype(np.float32).astype(np.int16).reshape(8, 16, W) for x in eff]; P = [x.astype(np.float32).astype(np.int16).reshape(8, 16, W) for x in req]
    S = [gentries(x).astype(np.int64).reshape(8, L, B) for x in act]; Q = [gentries(x).astype(np.int64).reshape(8, L, B) for x in why]
    s = [x.astype(np.float32).astype(np.int16).reshape(8, 16, B) for x in st0]; th = [gentries(x).astype(np.int64) for x in bar]; R = [0] * N
    for t in range(VI):
        v = [visit(E[r], P[r], S[r], Q[r], s[r], th[r], R[r], t) for r in range(N)]
        E = [x[3] for x in v]; R = [x[4] for x in v]; go = PS if t < VI - 1 else 0
        S = [v[(r - go) % N][0] for r in range(N)]; Q = [v[(r - go) % N][1] for r in range(N)]; s = [v[(r - 1) % N][2] for r in range(N)]
    return {"ys": np.stack([gtable(x.reshape(8, L * B)) for x in S]).astype(np.float32), "yw": np.stack([gtable(x.reshape(8, L * B)) for x in Q]).astype(np.float32),
            "ye": np.stack([x.reshape(128, W) for x in E]).astype(np.float32).astype(BF)}

@@ -1,0 +1,499 @@
+from concourse.mybir import AluOpType, AxisListType, ActivationFunctionType
+
+A = AluOpType
+ACT = ActivationFunctionType
+AX = AxisListType.X
+W, L, B, VI = 4096, 32, 128, 3
+PLAN_GO, STATE_GO = 3, 1
+H, F, I, U = "bfloat16", "float32", "int32", "uint16"
+
+SCRATCH = {}
+
+
+def _buf(dtype, n, *names):
+    for x in names:
+        SCRATCH[x] = ("sbuf", [128, n], dtype)
+
+
+_buf(H, W, "E", "PT", "TT", "ND", "Gc", "FL", "EC")
+_buf(H, 33 * B, "Gn", "D0", "D1", "V0")
+_buf(H, 2048, "SEL", "SEL2")
+_buf(H, 128, "ID", "ONE", "MK16", "SC0", "RM", "LT", "vx", "t12", "y", "Mb", "sv", "sq", "eb", "sc0", "sc1", "sc2", "so0", "so1")
+_buf(H, 8, "G8", "retb")
+_buf(H, 32, "ONES32")
+_buf(H, 512, "W4", "pp")
+_buf(H, 256, "o1", "eq", "e2p", "kept")
+_buf(F, 256, "K1c", "K19", "K2c", "K2", "prod1", "key2", "dfS", "dfQ")
+_buf(F, 32, "kc", "KAP")
+_buf(F, 512, "t64", "ysw")
+_buf(F, 8, "Cv", "Cn", "C32", "M8", "xf", "d8", "sxf", "bsf", "barf", "barM", "fnd", "nr", "cbr", "aq", "aqt")
+_buf(F, 24, "base24", "m24", "best24", "bar24", "ret24", "pr24", "a24")
+_buf(F, 16, "n16", "c16", "d16", "r16", "f16")
+_buf(F, 1, "rs", "thr")
+_buf(I, 2, "ri")
+_buf(I, 24, "oi24")
+_buf(I, 256, "craw", "cm")
+_buf(I, 512, "fin")
+_buf(I, 8, "M8i", "xr", "sx", "di", "dg", "Mdi", "sd", "pr0", "bs", "MBi", "cb", "ui", "ua", "uo")
+_buf(I, 16, "oi")
+_buf(I, 128, "vi", "e2", "es", "en")
+_buf(I, 264, "ZS", "ZQ", "tb")
+_buf(I, 256, "nS", "nQ")
+_buf(U, 512, "pl0", "pl1", "pl2", "plo0", "plo1")
+_buf(U, 256, "cu")
+_buf(U, 16, "ou")
+_buf(U, 8, "uu")
+for _b in range(8):
+    SCRATCH["ps%d" % _b] = ("psum", [128, 512], F)
+
+DMAS = ["ld%d" % k for k in range(12)] + ["ds%d" % k for k in range(3)]
+SEMAPHORES = ["qv", "qs", "qt", "qg"] + DMAS + ["ap1", "ap2", "as1", "as2", "lp1", "lp2", "ls1", "ls2"]
+
+
+def _tracker(g, T):
+    eng = {"v": g.vector, "s": g.scalar, "t": g.tensor, "g": g, "y": g.sync}
+    cnt, wr, rd, bank = {}, {}, {}, {}
+    known = {q: {} for q in eng}
+
+    def settle(q, toks):
+        best = {}
+        for sem, c, clk in toks:
+            if known[q].get(sem, 0) < c and (sem not in best or best[sem][0] < c):
+                best[sem] = (c, clk)
+        todo = sorted(best.items(), key=lambda x: -len(x[1][1]))
+        for sem, (c, clk) in todo:
+            if known[q].get(sem, 0) >= c:
+                continue
+            if any(s2 != sem and known[q].get(s2, 0) < c2 and k2.get(sem, 0) >= c for s2, (c2, k2) in todo):
+                continue
+            eng[q].wait_ge(T.sem[sem], c)
+            known[q][sem] = c
+            for s2, c2 in clk.items():
+                if known[q].get(s2, 0) < c2:
+                    known[q][s2] = c2
+
+    def note(q, tok, R, Wr, P):
+        for k in R:
+            rd.setdefault(k, []).append((q, tok))
+        for k in Wr:
+            wr[k] = (q, tok)
+            rd[k] = []
+        for b in P:
+            bank.setdefault(b, {})[q] = tok
+
+    def op(q, fn, R=(), Wr=(), P=(), sem=None, inc=1):
+        toks = []
+        for k in R:
+            if k in wr:
+                toks.append(wr[k][1])
+        for k in Wr:
+            if k in wr and not (q == "t" and wr[k][0] == "t"):
+                toks.append(wr[k][1])
+            toks += [t for q2, t in rd.get(k, []) if q2 != q or sem is not None]
+        for b in P:
+            toks += [t for q2, t in bank.get(b, {}).items() if q2 != q]
+        settle(q, toks)
+        ins = fn(eng[q])
+        name = sem or "q" + q
+        cnt[name] = cnt.get(name, 0) + inc
+        ins.then_inc(T.sem[name], inc)
+        note(q, (name, cnt[name], dict(known[q])), R, Wr, P)
+
+    def send(fn, R, local, n):
+        settle("g", [wr[k][1] for k in R])
+        fn()
+        cnt[local] = n
+        note("g", (local, n, dict(known["g"])), R, (), ())
+
+    def lands(sem, n, Wr):
+        cnt[sem] = n
+        note("x", (sem, n, {}), (), Wr, ())
+
+    def finish():
+        settle("g", [(s, c, {}) for s, c in cnt.items()])
+
+    return op, send, lands, finish
+
+
+def ks(x, n, a=0):
+    return [x + str(k) for k in range(a, n)]
+
+
+def rank_program(g, core, T, topo):
+    rank = T.rank_of(core)
+    if rank is None:
+        return
+    N = len(T.cores)
+    op, send, lands, finish = _tracker(g, T)
+
+    def ts(out, in0, s1, o0, s2=None, o1=None, R=(), Wr=(), P=()):
+        if o1 is None:
+            op("v", lambda e: e.tensor_scalar(out, in0, s1, None, o0), R, Wr, P)
+        else:
+            op("v", lambda e: e.tensor_scalar(out, in0, s1, s2, o0, o1), R, Wr, P)
+
+    def tt(out, a, b, o, R=(), Wr=(), P=()):
+        op("v", lambda e: e.tensor_tensor(out, a, b, o), R, Wr, P)
+
+    def cp(out, a, R=(), Wr=(), P=()):
+        op("v", lambda e: e.tensor_copy(out, a), R, Wr, P)
+
+    def fill(x, c, key=None):
+        op("v", lambda e: e.memset(x, c), (), [key or x.name])
+
+    def mm(out, l, r, start, stop, R, Wr, P):
+        op("t", lambda e: e.matmul(out, l, r, start, stop), R, Wr, P)
+
+    def act(out, a, fn, R, Wr, P=(), **kw):
+        op("s", lambda e: e.activation(out, a, fn, **kw), R, Wr, P)
+
+    def iota(out, pattern, base, cmul, key):
+        flag = {} if key in ("pi",) else {"allow_small_or_imprecise_dtypes": True}
+        op("g", lambda e: e.iota(out, pattern, base, cmul, **flag), (), [key])
+
+    def load(q, k, out, src, Wr):
+        op(q, lambda e: e.dma_start(out, src), (), Wr, (), "ld%d" % k, 16)
+
+    def gred(out, src, o, R, Wr, P=()):
+        for h in range(8):
+            op("v", lambda e, h=h: e.tensor_reduce(out[:, h:h + 1], src[:, h:256:8], AX, o), R, [Wr + str(h)], P)
+
+    load("s", 0, T.craw[:, :], T.act[:, :], ["ai"])
+    load("s", 1, T.cm[:, :], T.why[:, :], ["wi"])
+    load("s", 2, T.eb[:, :], T.st0[:, :], ["stin"])
+    load("s", 3, T.Mdi[:, :], T.bar[:, :], ["bari"])
+    for k in range(4):
+        load("y", 4 + k, T.E[:, k * 1024:k * 1024 + 1024], T.eff[:, k * 1024:k * 1024 + 1024], ["E%d" % k])
+    for k in range(4):
+        load("y", 8 + k, T.PT[:, k * 1024:k * 1024 + 1024], T.req[:, k * 1024:k * 1024 + 1024], ["P%d" % k])
+    EK = ks("E", 4)
+
+    fill(T.ONE[:, :], 1.0, "ONE")
+    op("g", lambda e: e.affine_select(T.ID[:, :], T.ONE[:, :], [[-1, 128]], A.is_equal, 0.0, 0, 1), ["ONE"], ["ID"])
+    op("g", lambda e: e.affine_select(T.G8[:, :], T.ONE[:, 0:8], [[-16, 8]], A.is_ge, 0.0, 0, 1), ["ONE"], ["G8"])
+    op("g", lambda e: e.affine_select(T.G8[:, :], T.G8[:, :], [[16, 8]], A.is_ge, 0.0, 15, -1), ["G8"], ["G8"])
+    iota(T.ui[:, :], [[0, 8]], 0, 1, "pi")
+    iota(T.kc[:, :], [[1, 32]], 0, 0, "kc")
+    iota(T.KAP[:, :], [[113, 32]], 37, 0, "KAP")
+    iota(T.K1c[:, :], [[-1, 32], [0, 8]], 32, 0, "K1c")
+    iota(T.K19[:, :], [[1, 32], [0, 8]], 0, 0, "K19")
+    iota(T.K2c[:, :], [[-4096, 32], [0, 8]], 31 * 4096, 0, "K2c")
+    iota(T.C32[:, :], [[16, 8]], 0, 0, "C32")
+    fill(T.SEL[:, :], 0.0, "SELz")
+    fill(T.SEL2[:, :], 0.0, "SEL2z")
+    fill(T.D0[:, 0:33 * B:33], -30000.0, "D0i")
+    fill(T.Gn[:, W:W + B], 192.0, "Gnx")
+    fill(T.ONES32[:, :], 1.0, "ONES32")
+    fill(T.SC0[:, :], -1000.0, "SC0z")
+    fill(T.SC0[:, 0:128:16], 1000.0, "SC0z")
+    fill(T.thr[:, :], 2.0, "thr")
+
+    cp(T.pl0[:, 0:256], T.craw[:, :], ["ai"], ["plS"])
+    ts(T.pl0[:, 256:512], T.cm[:, :], 2, A.add, R=["wi"], Wr=["plQ"])
+    ts(T.sq[:, :], T.eb[:, :], 8.0, A.is_ge, -264.0, A.mult, ["stin"], ["sq"])
+    tt(T.sc0[:, :], T.eb[:, :], T.sq[:, :], A.add, ["stin", "sq"], ["st"])
+
+    for c in range(8):
+        x = slice(c * 512, c * 512 + 512)
+        e = "E%d" % (c // 2)
+        ts(T.Gc[:, x], T.E[:, x], 4.0, A.is_ge, -520.0, A.mult, [e], ["Gc%d" % c])
+        ts(T.EC[:, x], T.E[:, x], 12.0, A.is_ge, 252.0, A.mult, [e], ["EC%d" % c])
+        p = T["ps%d" % (c % 4)]
+        bk = ["b%d" % (c % 4)]
+        pk = ["rg%d" % (c % 4)]
+        mm(p[:, :], T.ID[:, :], T.E[:, x], True, False, [e, "ID"], pk, bk)
+        mm(p[:, :], T.ID[:, :], T.Gc[:, x], False, False, ["Gc%d" % c], (), bk)
+        mm(p[:, :], T.ID[:, :], T.EC[:, x], False, True, ["EC%d" % c], pk, bk)
+        act(T.TT[:, x], p[:, :], ACT.Copy, pk, ["TT%d" % c], bk)
+    TK = ks("TT", 8)
+    for k in range(16):
+        cp(T.SEL[:, k * 128 + k:k * 128 + 128:16], T.G8[:, :], ["G8", "SELz"], ["SEL%d" % k])
+    ts(T.ua[:, :], T.ui[:, :], 15, A.bitwise_and, R=["pi"], Wr=["pb"])
+    tt(T.C32[:, :], T.C32[:, :], T.ua[:, :], A.add, ["C32", "pb"], ["C32"])
+    ts(T.Cv[:, :], T.C32[:, :], 33.0, A.mult, 32.0, A.add, ["C32"], ["Cv"])
+    ts(T.Cn[:, :], T.C32[:, :], 4096.0, A.add, R=["C32"], Wr=["Cn"])
+    ts(T.C32[:, :], T.C32[:, :], 32.0, A.mult, R=["C32", "Cv", "Cn"], Wr=["C32"])
+    ts(T.K1c[:, :], T.K1c[:, :], 262144.0, A.mult, R=["K1c"], Wr=["K1c"])
+    ts(T.K19[:, :], T.K19[:, :], 524288.0, A.mult, R=["K19"], Wr=["K19"])
+    cp(T.barf[:, :], T.Mdi[:, :], ["bari"], ["barf"])
+    for k in range(4):
+        x = slice(k * 1024, k * 1024 + 1024)
+        ts(T.ND[:, x], T.PT[:, x], 12.0, A.is_lt, R=["P%d" % k], Wr=["ND%d" % k])
+    NK = ks("ND", 4)
+    for k in range(16):
+        ts(T.SEL2[:, k * 128 + k:k * 128 + 128:16], T.G8[:, :], 131072.0, A.mult, R=["G8", "SEL2z"], Wr=["SEL2%d" % k])
+    tt(T.pp[:, 0:64], T.ID[:, 0:64], T.ID[:, 64:128], A.add, ["ID"], ["p1"])
+    tt(T.pp[:, 128:160], T.pp[:, 0:32], T.pp[:, 32:64], A.add, ["p1"], ["p2"])
+    tt(T.MK16[:, 0:16], T.pp[:, 128:144], T.pp[:, 144:160], A.add, ["p2"], ["MK16"])
+
+    for t in range(VI):
+        pl = T["pl%d" % t]
+        last = t == VI - 1
+        PLK = ["plS", "plQ"]
+        if t:
+            lands("ap%d" % t, len(topo.engines(T.cores[(rank - PLAN_GO) % N], core)), PLK)
+            lands("as%d" % t, len(topo.engines(T.cores[(rank - STATE_GO) % N], core)), ["st"])
+
+        def ab(c):
+            for k in range(4 * c, 4 * c + 4):
+                src = T.Gc[:, k * 128:k * 128 + 128]
+                ts(T.D1[:, k + 1:33 * B:33], src, 12.0 + 4 * k, A.add, R=["Gc%d" % c], Wr=["D1%d" % k])
+                ts(T.D0[:, k + 1:33 * B:33], src, -16.0, A.mult, -6400.0, A.add, ["Gc%d" % c], ["D0%d" % k])
+
+        def vgc(c):
+            cp(T.Gc[:, c * 512:c * 512 + 512], T.TT[:, :].indirect(pl[:, c * 32:c * 32 + 32]), TK + ["plS"], ["Gc%d" % c])
+
+        for c in range(6):
+            act(T.Gc[:, c * 512:c * 512 + 512], T.TT[:, :].indirect(pl[:, c * 32:c * 32 + 32]), ACT.Copy, TK + ["plS"], ["Gc%d" % c])
+        for c in range(8):
+            act(T.Gn[:, c * 512:c * 512 + 512], T.ND[:, :].indirect(pl[:, c * 32:c * 32 + 32]), ACT.Identity, NK + ["plS"], ["Gn%d" % c],
+                scale=188.0, bias=4.0)
+        vgc(7)
+        ts(T.D1[:, 0:33 * B:33], T["sc%d" % t][:, :], 4.0, A.add, R=["st"], Wr=["D1i"])
+        ab(7)
+        ab(0)
+        ab(1)
+        vgc(6)
+        ab(6)
+        for c in range(2, 6):
+            ab(c)
+        op("v", lambda e: e.tensor_tensor_scan(T.V0[:, :], T.D0[:, :], T.D1[:, :], 0.0, A.min, A.max),
+           ks("D0", 32) + ks("D1", 32) + ["D0i", "D1i"], ["V0"])
+        if t:
+            op("v", lambda e: e.tensor_reduce(T.rs[:, :], T.ps7[:, 280:288], AX, A.add), ["RS"], ["rs"], ["b7"])
+            cp(T.ri[:, 0:1], T.rs[:, :], ["rs"], ["ri"])
+            ts(T.ri[:, 1:2], T.ri[:, 0:1], 1, A.bitwise_and, R=["ri"], Wr=["rj"])
+            ts(T.thr[:, :], T.ri[:, 1:2], 2, A.add, R=["rj"], Wr=["thr"])
+
+        def ndps(c):
+            r = c % 4
+            mm(T["ps%d" % r][:, :], T.ID[:, :], T.Gn[:, c * 512:c * 512 + 512], True, True, ["ID", "Gn%d" % c], ["rg%d" % r], ["b%d" % r])
+
+        def flaw(c):
+            r = c % 4
+            for k in range(4 * c, 4 * c + 4):
+                tt(T.FL[:, k * 128:k * 128 + 128], T.V0[:, k:33 * B:33], T["ps%d" % r][:, (k % 4) * 128:(k % 4) * 128 + 128], A.is_ge,
+                   ["V0", "rg%d" % r], ["FL%d" % k], ["b%d" % r])
+
+        def count(src, key, sel, dst, bk, c, wk):
+            for k in range(16):
+                mm(dst[:, c * 64:c * 64 + 64], T[sel][:, k * 128:k * 128 + 128], src[:, c * 1024 + k:(c + 1) * 1024:16], k == 0, k == 15,
+                   ks(key, 8 * c + 8, 8 * c) + [sel + str(k)], [wk + str(c)] if k in (0, 15) else (), [bk])
+
+        for c in range(4):
+            ndps(c)
+        ts(T.t64[:, :], pl[:, :], 64.0, A.mult, R=PLK, Wr=["t64"])
+        tt(T.ps6[:, 0:256], T.t64[:, 0:256], T.K1c[:, :], A.add, ["t64", "K1c"], ["K1"], ["b6"])
+        flaw(0)
+        ndps(4)
+        flaw(1)
+        count(T.FL, "FL", "SEL", T.ps4, "b4", 0, "CN")
+        ndps(5)
+        flaw(2)
+        ndps(6)
+        flaw(3)
+        count(T.FL, "FL", "SEL", T.ps4, "b4", 1, "CN")
+        ndps(7)
+        for c in (4, 5):
+            flaw(c)
+        count(T.FL, "FL", "SEL", T.ps4, "b4", 2, "CN")
+        for c in (6, 7):
+            flaw(c)
+        count(T.FL, "FL", "SEL", T.ps4, "b4", 3, "CN")
+
+        v32 = T.V0[:, 32:33 * B:33]
+        for k, (cut, o, s) in enumerate(((0.0, A.is_lt, 12.0), (-248.0, A.is_lt, -4.0), (8.0, A.is_ge, 4.0), (12.0, A.is_ge, -4.0))):
+            ts(T.pp[:, k * 128:k * 128 + 128], v32, cut, o, s, A.mult, ["V0"], ["p%d" % (k + 1)])
+        for k in range(4):
+            mm(T.ps5[:, 256:384], T.ID[:, :], T.pp[:, k * 128:k * 128 + 128], k == 0, k == 3, ["ID", "p%d" % (k + 1)], ["SP"] if k in (0, 3) else (), ["b5"])
+        cp(T.vi[:, :], v32, ["V0"], ["vi"])
+        ts(T.e2[:, :], T.vi[:, :], 3, A.bitwise_and, R=["vi"], Wr=["e2"])
+
+        ts(T.o1[:, :], T.ps4[:, 0:256], T.thr[:, :], A.is_ge, R=ks("CN", 4) + ["thr"], Wr=["o1"], P=["b4"])
+        tt(T.prod1[:, :], T.o1[:, :], T.ps6[:, 0:256], A.mult, ["o1", "K1"], ["prod1"], ["b6"])
+        gred(T.M8, T.prod1, A.max, ["prod1"], "M8")
+        cp(T.M8i[:, :], T.M8[:, :], ks("M8", 8), ["M8i"])
+        ts(T.xr[:, :], T.M8i[:, :], 18, A.arith_shift_right, R=["M8i"], Wr=["xr"])
+        ts(T.sx[:, :], T.M8i[:, :], 6, A.arith_shift_right, 4095, A.bitwise_and, ["M8i"], ["sx"])
+        ts(T.n16[:, 0:8], T.xr[:, :], -128.0, A.mult, R=["xr"], Wr=["xm"])
+        tt(T.oi[:, 0:8], T.Cv[:, :], T.xr[:, :], A.subtract, ["Cv", "xr"], ["oi0"])
+        tt(T.oi[:, 8:16], T.Cn[:, :], T.n16[:, 0:8], A.add, ["Cn", "xm"], ["oi1"])
+        cp(T.ou[:, :], T.oi[:, :], ["oi0", "oi1"], ["ou"])
+        GNK = ks("Gn", 8) + ["Gnx"]
+        act(T.vx[:, :], T.V0[:, :].indirect(T.ou[:, 0:8]), ACT.Copy, ["V0", "ou"], ["vx"])
+        ts(T.t12[:, :], T.V0[:, :].indirect(T.ou[:, 0:8]), 0.0, A.is_ge, 12.0, A.mult, ["V0", "ou"], ["t12"])
+        tt(T.y[:, :], T.Gn[:, :].indirect(T.ou[:, 8:16]), T.vx[:, :], A.subtract, GNK + ["ou", "vx"], ["y"])
+        mm(T.ps7[:, 0:128], T.y[:, :], T.ID[:, :], True, True, ["y", "ID"], ["DT"], ["b7"])
+        tt(T.W4[:, 0:128], T.Gn[:, :].indirect(T.ou[:, 8:16]), T.t12[:, :], A.max, GNK + ["ou", "t12"], ["W4a"])
+        op("v", lambda e: e.tensor_tensor_scan(T.RM[:, :], T.SC0[:, :], T.ps7[:, 0:128], 0.0, A.max, A.min), ["SC0z", "DT"], ["RM"], ["b7"])
+        for h in range(8):
+            ts(T.LT[:, h * 16:h * 16 + 16], T.MK16[:, 0:16], T.RM[:, h * 16 + 15:h * 16 + 16], A.mult, R=["MK16", "RM"], Wr=["LT%d" % h])
+        mm(T.ps7[:, 256:264], T.LT[:, :], T.G8[:, :], True, True, ks("LT", 8) + ["G8"], ["D8"], ["b7"])
+        for k in range(4):
+            mm(T.ps0[:, k * 128:k * 128 + 128], T.ID[:, :], T.W4[:, 0:128], True, True, ["ID", "W4a"], ["rg0"], ["b0"])
+        ts(T.xf[:, :], T.xr[:, :], -1.0, A.mult, 32.0, A.add, ["xr"], ["xf"])
+        ts(T.di[:, :], T.ps7[:, 256:264], -1.0, A.mult, -8.0, A.add, ["D8"], ["di"], ["b7"])
+        ts(T.dg[:, :], T.di[:, :], 2, A.arith_shift_right, 63, A.bitwise_and, ["di"], ["dg"])
+        tt(T.d8[:, :], T.dg[:, :], T.xf[:, :], A.min, ["dg", "xf"], ["d8"])
+        for h in range(8):
+            ts(T.eq[:, h:256:8], T.kc[:, :], T.d8[:, h:h + 1], A.is_equal, R=["kc", "d8"], Wr=["eq%d" % h])
+        tt(T.prod1[:, :], T.eq[:, :], T.ps6[:, 0:256], A.mult, ks("eq", 8) + ["K1"], ["prod1"], ["b6"])
+        gred(T.M8, T.prod1, A.max, ["prod1"], "M8")
+        cp(T.Mdi[:, :], T.M8[:, :], ks("M8", 8), ["Mdi"])
+        ts(T.sd[:, :], T.Mdi[:, :], 6, A.arith_shift_right, 4095, A.bitwise_and, ["Mdi"], ["sd"])
+        tt(T.pr0[:, :], T.sx[:, :], T.sd[:, :], A.mult, ["sx", "sd"], ["pr0"])
+        cp(T.sxf[:, :], T.sx[:, :], ["sx"], ["sxf"])
+        if t:
+            ts(T.pr0[:, :], T.pr0[:, :], 32.0 * 97 * t, A.add, R=["pr0"], Wr=["pr0"])
+        ts(T.bs[:, :], T.pr0[:, :], 5, A.arith_shift_right, R=["pr0"], Wr=["bs"])
+        cp(T.bsf[:, :], T.bs[:, :], ["bs"], ["bsf"])
+        for h in range(8):
+            ts(T.craw[:, h:256:8], T.KAP[:, :], T.sxf[:, h:h + 1], A.mult, T.bsf[:, h:h + 1], A.add, ["KAP", "sxf", "bsf"], ["craw%d" % h])
+        ts(T.cm[:, :], T.craw[:, :], 4095, A.bitwise_and, R=ks("craw", 8), Wr=["cm"])
+        cp(T.cu[:, :], T.cm[:, :], ["cm"], ["cu"])
+
+        for c in range(6):
+            act(T.EC[:, c * 512:c * 512 + 512], T.E[:, :].indirect(T.cu[:, c * 32:c * 32 + 32]), ACT.Copy, EK + ["cu"], ["EC%d" % c])
+        for k in range(1, 4):
+            cp(T.W4[:, k * 128:k * 128 + 128], T.W4[:, 0:128], ["W4a"], ["W4%d" % k])
+
+        def vfuse(c):
+            tt(T.FL[:, c * 512:c * 512 + 512], T.E[:, :].indirect(T.cu[:, c * 32:c * 32 + 32]), T.W4[:, :], A.is_ge,
+               EK + ["cu", "W4a"] + ks("W4", 4, 1), ks("FL", 4 * c + 4, 4 * c))
+
+        def hit(c):
+            tt(T.FL[:, c * 512:c * 512 + 512], T.EC[:, c * 512:c * 512 + 512], T.ps0[:, :], A.is_ge, ["EC%d" % c, "rg0"], ks("FL", 4 * c + 4, 4 * c), ["b0"])
+
+        def score(c):
+            count(T.FL, "FL", "SEL2", T.ps4, "b4", c, "CN")
+
+        vfuse(7)
+        tt(T.sv[:, :], T.e2[:, :], T.ps5[:, 256:384], A.add, ["e2", "SP"], ["sv"], ["b5"])
+        ts(T.Mb[:, :], T.W4[:, 0:128], 4.0, A.is_equal, R=["W4a"], Wr=["Mb"])
+        hit(0)
+        for k in range(16):
+            mm(T.ps7[:, 272:280], T.SEL[:, k * 128:k * 128 + 128], T.sv[:, k:128:16], k == 0, k == 15, ["sv", "SEL%d" % k], ["U8"] if k in (0, 15) else (), ["b7"])
+        for k in range(16):
+            mm(T.ps5[:, 0:8], T.SEL[:, k * 128:k * 128 + 128], T.Mb[:, k:128:16], k == 0, k == 15, ["Mb", "SEL%d" % k], ["NM"] if k in (0, 15) else (), ["b5"])
+        if not last:
+            so = T["so%d" % t]
+            ts(T.sq[:, :], T.sv[:, :], 8.0, A.is_ge, -264.0, A.mult, ["sv"], ["sq"])
+            tt(so[:, :], T.sv[:, :], T.sq[:, :], A.add, ["sv", "sq"], ["so"])
+            dst = T.cores[(rank + STATE_GO) % N]
+            rid, pid, _ = topo.addr(dst)
+            n = len(topo.engines(core, dst))
+            send(lambda: g.remote_dma(T["sc%d" % (t + 1)][:, :], so[:, :], T.sem["as%d" % (t + 1)], T.sem["ls%d" % (t + 1)], pid, rid, topo.mask(core, dst)),
+                 ["so"], "ls%d" % (t + 1), n)
+        hit(1)
+        score(0)
+        vfuse(6)
+        score(3)
+        tt(T.K2[:, :], T.K2c[:, :], T.cm[:, :], A.add, ["K2c", "cm"], ["K2"])
+        hit(2)
+        for k in range(2):
+            cp(T.base24[:, k * 8:k * 8 + 8], T.xf[:, :], ["xf"], ["ba%d" % k])
+        if t == 0:
+            fill(T.base24[:, 16:24], 0.0, "ba2")
+        ts(T.m24[:, 0:8], T.xf[:, :], -1.0, A.mult, 99.0, A.add, ["xf"], ["m240"])
+        tt(T.m24[:, 8:16], T.d8[:, :], T.xf[:, :], A.subtract, ["d8", "xf"], ["m241"])
+        ts(T.m24[:, 16:24], T.sd[:, :], 64.0, A.mult, 128.0, A.add, ["sd"], ["m242"])
+        ts(T.fnd[:, :], T.xr[:, :], 1.0, A.is_ge, R=["xr"], Wr=["fnd"])
+        tt(T.barM[:, :], T.barf[:, :], T.ps5[:, 0:8], A.add, ["barf", "NM"], ["barM"], ["b5"])
+        hit(3)
+        score(1)
+        for k in range(3):
+            tt(T.bar24[:, k * 8:k * 8 + 8], T.barM[:, :], T.fnd[:, :], A.mult, ["barM", "fnd"], ["br%d" % k])
+        hit(4)
+        cp(T.ui[:, :], T.ps7[:, 272:280], ["U8"], ["ui"], ["b7"])
+        ts(T.ua[:, :], T.ui[:, :], 31, A.bitwise_and, R=["ui"], Wr=["ua"])
+        tt(T.uo[:, :], T.ua[:, :], T.C32[:, :], A.add, ["ua", "C32"], ["uo"])
+        cp(T.uu[:, :], T.uo[:, :], ["uo"], ["uu"])
+        hit(5)
+        score(2)
+        tt(T.es[:, :], T.E[:, :].indirect(T.uu[:, :]), T.sv[:, :], A.add, EK + ["uu", "sv"], ["es"])
+        ts(T.en[:, :], T.es[:, :], 1, A.arith_shift_right, R=["es"], Wr=["en"])
+        cp(T.eb[:, :], T.en[:, :], ["en"], ["eb"])
+        op("v", lambda e: e.tensor_copy(T.E[:, :].indirect(T.uu[:, :]), T.eb[:, :]), ["eb", "uu"], EK)
+        if last:
+            op("y", lambda e: e.dma_start(T.ye[:, :], T.E[:, :]), EK, ["ye"], (), "ds0", 16)
+
+        tt(T.key2[:, :], T.K2[:, :], T.ps4[:, 0:256], A.add, ["K2"] + ks("CN", 4), ["key2"], ["b4"])
+        gred(T.M8, T.key2, A.max, ["key2"], "M8")
+        cp(T.MBi[:, :], T.M8[:, :], ks("M8", 8), ["MBi"])
+        for k in range(3):
+            op("v", lambda e, k=k: e.tensor_scalar(T.oi24[:, k * 8:k * 8 + 8], T.MBi[:, :], 17, None, A.arith_shift_right), ["MBi"], ["bt%d" % k])
+        ts(T.cb[:, :], T.MBi[:, :], 4095, A.bitwise_and, R=["MBi"], Wr=["cb"])
+        tt(T.ret24[:, :], T.oi24[:, :], T.bar24[:, :], A.is_lt, ks("bt", 3) + ks("br", 3), ["ret"])
+        tt(T.pr24[:, :], T.ret24[:, :], T.m24[:, :], A.mult, ["ret"] + ks("m24", 3), ["pr24"])
+        tt(T.a24[:, :], T.base24[:, :], T.pr24[:, :], A.add, ["pr24"] + ks("ba", 3), ["a24"])
+        for h in range(8):
+            ts(T.ps0[:, h:256:8], T.kc[:, :], T.a24[:, h:h + 1], A.min, T.a24[:, 8 + h:9 + h], A.not_equal, ["kc", "a24"], ["e1%d" % h], ["b0"])
+            ts(T.e2p[:, h:256:8], T.t64[:, 256 + h:512:8], T.a24[:, 16 + h:17 + h], A.not_equal, R=["t64", "a24"], Wr=["e2p%d" % h])
+        tt(T.kept[:, :], T.e2p[:, :], T.ps0[:, 0:256], A.min, ks("e1", 8) + ks("e2p", 8), ["kept"], ["b0"])
+        if not last:
+            cp(T.retb[:, :], T.ret24[:, 0:8], ["ret"], ["retb"])
+            mm(T.ps7[:, 280:288], T.ONE[:, :], T.retb[:, :], True, True, ["ONE", "retb"], ["RS"], ["b7"])
+        for h in range(8):
+            op("v", lambda e, h=h: e.tensor_tensor_scan(T.ps1[:, h:256:8], T.ONES32[:, :], T.kept[:, h:256:8], 1.0, A.add, A.subtract),
+               ["ONES32", "kept"], ["sp%d" % h], ["b1"])
+        tt(T.ps1[:, 256:512], T.kept[:, :], T.ps1[:, 0:256], A.mult, ["kept"] + ks("sp", 8), ["shk"], ["b1"])
+        op("v", lambda e: e.memset(T.ZS[:, 0:8], 0), (), ["ZS0"])
+        op("v", lambda e: e.memset(T.ZQ[:, 0:8], 0), (), ["ZQ0"])
+        tt(T.ps0[:, 256:512], T.K19[:, :], T.ps1[:, 256:512], A.add, ["K19", "shk"], ["ksh"], ["b0", "b1"])
+        tt(T.ZS[:, 8:264], T.t64[:, 0:256], T.ps0[:, 256:512], A.add, ["t64", "ksh"], ["ZS"], ["b0"])
+        tt(T.ZQ[:, 8:264], T.t64[:, 256:512], T.ps0[:, 256:512], A.add, ["t64", "ksh"], ["ZQ"], ["b0"])
+        for k in range(2):
+            ts(T.n16[:, k * 8:k * 8 + 8], T.ps1[:, 248:256], -1.0, A.mult, 33.0, A.add, ks("sp", 8), ["n16%d" % k, "xm"], ["b1"])
+        if t == 0:
+            fill(T.c16[:, 0:8], 99.0, "c160")
+        cp(T.c16[:, 8:16], T.xf[:, :], ["xf"], ["c161"])
+        ts(T.nr[:, :], T.ret24[:, 0:8], -1.0, A.mult, 1.0, A.add, ["ret"], ["nr"])
+        ts(T.aqt[:, :], T.sd[:, :], 1.0, A.add, R=["sd"], Wr=["aqt"])
+        tt(T.d16[:, :], T.n16[:, :], T.c16[:, :], A.subtract, ["n160", "n161", "c160", "c161"], ["d16"])
+        tt(T.cbr[:, :], T.cb[:, :], T.nr[:, :], A.mult, ["cb", "nr"], ["cbr"])
+        tt(T.aq[:, :], T.aqt[:, :], T.nr[:, :], A.mult, ["aqt", "nr"], ["aq0"])
+        tt(T.r16[:, :], T.d16[:, :], T.ret24[:, 0:16], A.mult, ["d16", "ret"], ["r16"])
+        ts(T.aq[:, :], T.aq[:, :], 1.0, A.add, R=["aq0"], Wr=["aq"])
+        tt(T.f16[:, :], T.r16[:, :], T.c16[:, :], A.add, ["r16", "c160", "c161"], ["f16"])
+        for h in range(8):
+            ts(T.ps1[:, h:256:8], T.cm[:, h:256:8], T.ret24[:, h:h + 1], A.mult, T.cbr[:, h:h + 1], A.add, ["cm", "ret", "cbr"], ["al%d" % h, "sp%d" % h], ["b1"])
+        for h in range(8):
+            ts(T.ps0[:, h:256:8], T.kc[:, :], T.f16[:, h:h + 1], A.min, T.f16[:, 8 + h:9 + h], A.is_equal, ["kc", "f16"], ["Fp%d" % h, "e1%d" % h], ["b0"])
+        for b in range(6):
+            s = 1 << b
+            m = (33 - s) * 8
+            z = ["ZS", "ZS0"]
+            q = ["ZQ", "ZQ0"]
+            ts(T.tb[:, 0:m], T.ZS[:, 8 * s:264], b, A.arith_shift_right, 1, A.bitwise_and, z, ["tb"])
+            tt(T.ps3[:, 0:m], T.tb[:, 0:m], T.ZQ[:, 8 * s:264], A.mult, ["tb"] + q, ["mvQ"], ["b3"])
+            tt(T.ps2[:, 0:m], T.tb[:, 0:m], T.ZS[:, 8 * s:264], A.mult, ["tb"] + z, ["mvS"], ["b2"])
+            tt(T.ZQ[:, 0:m], T.ZQ[:, 0:m], T.ps3[:, 0:m], A.max, q + ["mvQ"], q, ["b3"])
+            tt(T.ZS[:, 0:m], T.ZS[:, 0:m], T.ps2[:, 0:m], A.max, z + ["mvS"], z, ["b2"])
+        ts(T.nQ[:, :], T.ZQ[:, 0:256], 6, A.arith_shift_right, 8191, A.bitwise_and, ["ZQ", "ZQ0"], ["nQ"])
+        ts(T.nS[:, :], T.ZS[:, 0:256], 6, A.arith_shift_right, 8191, A.bitwise_and, ["ZS", "ZS0"], ["nS"])
+        for h in range(8):
+            ts(T.dfQ[:, h:256:8], T.nQ[:, h:256:8], -1.0, A.mult, T.aq[:, h:h + 1], A.add, ["nQ", "aq"], ["dfQ%d" % h])
+        tt(T.dfS[:, :], T.ps1[:, 0:256], T.nS[:, :], A.subtract, ks("al", 8) + ["nS"], ["dfS"], ["b1"])
+        tt(T.ps3[:, 0:256], T.dfQ[:, :], T.ps0[:, 0:256], A.mult, ks("dfQ", 8) + ks("Fp", 8), ["mvQ"], ["b3", "b0"])
+        tt(T.ps2[:, 0:256], T.dfS[:, :], T.ps0[:, 0:256], A.mult, ["dfS"] + ks("Fp", 8), ["mvS"], ["b2", "b0"])
+        if not last:
+            tt(T.fin[:, 256:512], T.nQ[:, :], T.ps3[:, 0:256], A.add, ["nQ", "mvQ"], ["finQ"], ["b3"])
+            tt(T.fin[:, 0:256], T.nS[:, :], T.ps2[:, 0:256], A.add, ["nS", "mvS"], ["finS"], ["b2"])
+            po = T["plo%d" % t]
+            cp(po[:, :], T.fin[:, :], ["finS", "finQ"], ["po"])
+            dst = T.cores[(rank + PLAN_GO) % N]
+            rid, pid, _ = topo.addr(dst)
+            n = len(topo.engines(core, dst))
+            send(lambda: g.remote_dma(T["pl%d" % (t + 1)][:, :], po[:, :], T.sem["ap%d" % (t + 1)], T.sem["lp%d" % (t + 1)], pid, rid, topo.mask(core, dst)),
+                 ["po"], "lp%d" % (t + 1), n)
+            ts(T.pp[:, 0:128], T.eb[:, :], 4.0, A.is_ge, -520.0, A.mult, ["eb"], ["p1"])
+            ts(T.pp[:, 128:256], T.eb[:, :], 12.0, A.is_ge, 252.0, A.mult, ["eb"], ["p2"])
+            tt(T.pp[:, 256:384], T.pp[:, 0:128], T.pp[:, 128:256], A.add, ["p1", "p2"], ["p3"])
+            tt(T.TT[:, :].indirect(T.uu[:, :]), T.eb[:, :], T.pp[:, 256:384], A.add, ["eb", "p3", "uu"], TK)
+        else:
+            tt(T.ysw[:, 0:256], T.nS[:, :], T.ps2[:, 0:256], A.add, ["nS", "mvS"], ["ysw0"], ["b2"])
+            op("y", lambda e: e.dma_start(T.ys[:, :], T.ysw[:, 0:256]), ["ysw0"], ["ys"], (), "ds1", 16)
+            tt(T.dfQ[:, :], T.nQ[:, :], T.ps3[:, 0:256], A.add, ["nQ", "mvQ"] + ks("dfQ", 8), ["dfQ"], ["b3"])
+            ts(T.ysw[:, 256:512], T.dfQ[:, :], 2.0, A.subtract, R=["dfQ"], Wr=["ysw1"])
+            op("s", lambda e: e.dma_start(T.yw[:, :], T.ysw[:, 256:512]), ["ysw1"], ["yw"], (), "ds2", 16)
+    finish()

@@ -18,26 +18,26 @@ def _buf(dtype, n, *names):
 _buf(H, W, "E", "PT", "TT", "ND", "Gc", "FL", "EC")
 _buf(H, 33 * B, "Gn", "D0", "D1", "V0")
 _buf(H, 2048, "SEL", "SEL2")
-_buf(H, 128, "ID", "ONE", "MK16", "SC0", "RM", "LT", "vx", "t12", "y", "Mb", "sv", "sq", "eb", "sc0", "sc1", "sc2", "so0", "so1")
+_buf(H, 128, "ID", "ONE", "MK16", "SC0", "FOUR", "LT", "vx", "t12", "y", "Mb", "sv", "sq", "eb", "sc0", "sc1", "sc2", "so0", "so1")
 _buf(H, 8, "G8", "retb")
 _buf(H, 32, "ONES32")
-_buf(H, 512, "W4", "pp")
-_buf(H, 256, "o1", "eq", "e2p", "kept")
-_buf(F, 256, "K1c", "K19", "K2c", "K2", "prod1", "key2", "dfS", "dfQ")
+_buf(H, 512, "W4", "pp", "IS")
+_buf(F, 128, "RM")
+_buf(H, 256, "o1", "kept")
+_buf(F, 256, "K1c", "K19", "K18", "K2c", "K2", "prod1", "key2", "cm64", "t64", "t64S")
 _buf(F, 32, "kc", "KAP")
-_buf(F, 512, "t64", "ysw")
-_buf(F, 8, "Cv", "Cn", "C32", "M8", "xf", "d8", "sxf", "bsf", "barf", "barM", "fnd", "nr", "cbr", "aq", "aqt")
+_buf(F, 512, "ysw")
+_buf(F, 8, "Cv", "Cn", "C32", "SG", "ncd", "xf", "d8", "sxf", "bsf", "barf", "barM", "fnd", "nr", "cbx", "cbr", "aq", "aqt")
 _buf(F, 24, "base24", "m24", "best24", "bar24", "ret24", "pr24", "a24")
 _buf(F, 16, "n16", "c16", "d16", "r16", "f16")
 _buf(F, 1, "rs", "thr")
 _buf(I, 2, "ri")
-_buf(I, 24, "oi24")
+_buf(I, 6 * 264, "tb")
 _buf(I, 256, "craw", "cm")
-_buf(I, 512, "fin")
-_buf(I, 8, "M8i", "xr", "sx", "di", "dg", "Mdi", "sd", "pr0", "bs", "MBi", "cb", "ui", "ua", "uo")
+_buf(I, 8, "M8i", "xr", "xm", "sx", "di", "dg", "Mdi", "sd", "pr0", "bs", "MBi", "cb", "ui", "ua", "uo")
 _buf(I, 16, "oi")
 _buf(I, 128, "vi", "e2", "es", "en")
-_buf(I, 264, "ZS", "ZQ", "tb")
+_buf(I, 264, "ZS", "ZQ")
 _buf(I, 256, "nS", "nQ")
 _buf(U, 512, "pl0", "pl1", "pl2", "plo0", "plo1")
 _buf(U, 256, "cu")
@@ -47,12 +47,16 @@ for _b in range(8):
     SCRATCH["ps%d" % _b] = ("psum", [128, 512], F)
 
 DMAS = ["ld%d" % k for k in range(12)] + ["ds%d" % k for k in range(3)]
-SEMAPHORES = ["qv", "qs", "qt", "qg"] + DMAS + ["ap1", "ap2", "as1", "as2", "lp1", "lp2", "ls1", "ls2"]
+SEMAPHORES = ["qv", "qs", "qt", "qg"] + DMAS + ["ap1", "ap2", "aq1", "aq2", "as1", "as2", "lp1", "lp2", "lq1", "lq2", "ls1", "ls2"]
+NSC = 6
+EARLY = True
+NVD = 1
+NVG = 14
 
 
 def _tracker(g, T):
     eng = {"v": g.vector, "s": g.scalar, "t": g.tensor, "g": g, "y": g.sync}
-    cnt, wr, rd, bank = {}, {}, {}, {}
+    cnt, bank = {}, {}
     known = {q: {} for q in eng}
 
     def settle(q, toks):
@@ -72,47 +76,159 @@ def _tracker(g, T):
                 if known[q].get(s2, 0) < c2:
                     known[q][s2] = c2
 
-    def note(q, tok, R, Wr, P):
-        for k in R:
-            rd.setdefault(k, []).append((q, tok))
-        for k in Wr:
-            wr[k] = (q, tok)
-            rd[k] = []
+    def op(q, fn, toks, P, sem, inc):
         for b in P:
-            bank.setdefault(b, {})[q] = tok
-
-    def op(q, fn, R=(), Wr=(), P=(), sem=None, inc=1):
-        toks = []
-        for k in R:
-            if k in wr:
-                toks.append(wr[k][1])
-        for k in Wr:
-            if k in wr and not (q == "t" and wr[k][0] == "t"):
-                toks.append(wr[k][1])
-            toks += [t for q2, t in rd.get(k, []) if q2 != q or sem is not None]
-        for b in P:
-            toks += [t for q2, t in bank.get(b, {}).items() if q2 != q]
+            toks = toks + [t for q2, t in bank.get(b, {}).items() if q2 != q]
         settle(q, toks)
         ins = fn(eng[q])
         name = sem or "q" + q
         cnt[name] = cnt.get(name, 0) + inc
         ins.then_inc(T.sem[name], inc)
-        note(q, (name, cnt[name], dict(known[q])), R, Wr, P)
+        tok = (name, cnt[name], dict(known[q]))
+        for b in P:
+            bank.setdefault(b, {})[q] = tok
+        return tok
 
-    def send(fn, R, local, n):
-        settle("g", [wr[k][1] for k in R])
+    def send(fn, toks, local, n):
+        settle("g", toks)
         fn()
         cnt[local] = n
-        note("g", (local, n, dict(known["g"])), R, (), ())
+        return (local, n, dict(known["g"]))
 
-    def lands(sem, n, Wr):
+    def lands(sem, n):
         cnt[sem] = n
-        note("x", (sem, n, {}), (), Wr, ())
+        return (sem, n, {})
 
     def finish():
         settle("g", [(s, c, {}) for s, c in cnt.items()])
 
     return op, send, lands, finish
+
+
+SHARED = (("Sf", "K2", "dfS", "al"), ("prod1", "df", "dfQ"), ("key2", "kss"), ("o1", "e2p"), ("aqt", "dxs"), ("rg0", "e1", "ksh", "Fp"),
+          ("rg1", "sp", "shk", "alY"), ("rg2", "mvS"), ("rg3", "mvQ"), ("stin", "eb"), ("ai", "craw"), ("wi", "cm"), ("pi", "ui"), ("pb", "ua"), ("fx", "FL"), ("aq0", "aq"))
+TAKES = {"v": {"V0": 1.75, "y": .25, "W4a": .25, "t12": .25, "RM": .11, "es": .25, "eb": .11, "en": .11, "E": .42, "TT": .42, "sv": .11, "vi": .11, "e2": .11, "FL": .11,
+               "Gc": .21, "EC": .21, "fx": .21, "ND": .43, "LT": .053, "D": .053},
+         "s": {"Gc": .7, "Gn": .7, "EC": .7, "vx": .25, "TT": .43}, "t": {"rg": .43, "SP": .11, "DT": .11}}
+for _k in ("o1", "prod1", "K1", "kss", "cm64", "alY", "Sf", "t64S", "t64Q", "cm", "cu", "K2", "key2", "kept", "shk", "ksh", "ZS", "ZQ", "tb", "mvS", "mvQ", "nS", "nQ", "dfS", "fin",
+           "po", "ysw", "so"):
+    TAKES["v"][_k] = .2
+WAKE = 0.15
+REORDER = ("v",)
+
+
+def _takes(e):
+    kind, q, Wr = e[0], e[1], e[4]
+    if kind == "send":
+        return 0.5
+    if kind == "lands":
+        return 2.0
+    if e[6] is not None:
+        return 0.05
+    if q == "v" and len(Wr) == 4 and Wr[0].startswith("FL"):
+        return 0.7 if "cu" in e[3] else 0.43
+    if "plS" in e[3] and Wr[0].startswith("D1"):
+        return 0.22
+    if "plS" in e[3] and Wr[0].startswith("Gn"):
+        return 0.7
+    k = Wr[0] if Wr else ""
+    tab = TAKES.get(q, {})
+    return tab.get(k, tab.get(k.rstrip("0123456789"), .06 if q != "g" else .3))
+
+
+def _schedule(prog):
+    fam = {}
+    for f in SHARED:
+        for s in f:
+            fam[s] = f
+    stem = {}
+
+    def st(k):
+        if k not in stem:
+            stem[k] = k if k in fam else k.rstrip("0123456789")
+        return stem[k]
+
+    wr, rd, keys = {}, {}, {}
+    deps = []
+    for i, e in enumerate(prog):
+        d = set()
+        for k in e[3]:
+            if k in wr:
+                d.add(wr[k])
+        for k in e[4]:
+            if k in wr:
+                d.add(wr[k])
+            d.update(rd.get(k, ()))
+            for s in fam.get(st(k), ()):
+                if s != st(k):
+                    for k2 in keys.get(s, ()):
+                        if k2 in wr:
+                            d.add(wr[k2])
+                        d.update(rd.get(k2, ()))
+        for k in e[3]:
+            rd.setdefault(k, []).append(i)
+            keys.setdefault(st(k), set()).add(k)
+        for k in e[4]:
+            wr[k] = i
+            rd[k] = []
+            keys.setdefault(st(k), set()).add(k)
+        d.discard(i)
+        deps.append(d)
+    n = len(prog)
+    cost = [_takes(e) for e in prog]
+    nxt = [[] for _ in range(n)]
+    for i in range(n):
+        for j in deps[i]:
+            nxt[j].append(i)
+    rank = [0.0] * n
+    for i in range(n - 1, -1, -1):
+        m = 0.0
+        for j in nxt[i]:
+            m = max(m, rank[j] + WAKE)
+        lat = 5.0 if prog[i][6] is not None else 0.0
+        rank[i] = cost[i] + lat + m
+    left = [len(d) for d in deps]
+    ready = {}
+    fifo = {}
+    for i, e in enumerate(prog):
+        if e[1] not in REORDER and e[1] != "x":
+            fifo.setdefault(e[1], []).append(i)
+    head = {q: 0 for q in fifo}
+    at = [0.0] * n
+    free = {}
+    for i in range(n):
+        if not left[i]:
+            ready.setdefault(prog[i][1], set()).add(i)
+    order = []
+    while len(order) < n:
+        pick = None
+        for q, r in ready.items():
+            c = r
+            if q in fifo:
+                i = fifo[q][head[q]] if head[q] < len(fifo[q]) else None
+                c = (i,) if i in r else ()
+            if not c:
+                continue
+            f = free.get(q, 0.0) if q != "x" else 0.0
+            t0 = min(max(f, at[i]) for i in c)
+            b = min((-rank[i], i) for i in c if max(f, at[i]) <= t0 + 0.02)[1]
+            s = max(f, at[b])
+            if pick is None or s < pick[0]:
+                pick = (s, b, q)
+        s, i, q = pick
+        ready[q].discard(i)
+        if q in head:
+            head[q] += 1
+        end = s + cost[i]
+        free[q] = end
+        order.append((s, i))
+        lat = 5.0 if prog[i][6] is not None else 0.0
+        for j in nxt[i]:
+            at[j] = max(at[j], end + lat + WAKE)
+            left[j] -= 1
+            if not left[j]:
+                ready.setdefault(prog[j][1], set()).add(j)
+    return [i for _, i in order], deps
 
 
 def ks(x, n, a=0):
@@ -124,7 +240,21 @@ def rank_program(g, core, T, topo):
     if rank is None:
         return
     N = len(T.cores)
-    op, send, lands, finish = _tracker(g, T)
+    op_now, send_now, lands_now, finish = _tracker(g, T)
+    prog = []
+
+    def op(q, fn, R=(), Wr=(), P=(), sem=None, inc=1):
+        prog.append(("op", q, fn, tuple(R), tuple(Wr), tuple(P), sem, inc))
+
+    def send(fn, R, local, n):
+        prog.append(("send", "g", fn, tuple(R), ("@" + local[1:] + "x",), (), None, (local, n)))
+
+    def lands(sem, n, Wr):
+        prog.append(("lands", "x", None, ("@" + sem[1:] + "x",), tuple(Wr), (), None, (sem, n)))
+
+    def remote(out, src, there, here, dst):
+        rid, pid, _ = topo.addr(dst)
+        return lambda: g.remote_dma(out, src, T.sem[there], T.sem[here], pid, rid, topo.mask(core, dst))
 
     def ts(out, in0, s1, o0, s2=None, o1=None, R=(), Wr=(), P=()):
         if o1 is None:
@@ -137,6 +267,9 @@ def rank_program(g, core, T, topo):
 
     def cp(out, a, R=(), Wr=(), P=()):
         op("v", lambda e: e.tensor_copy(out, a), R, Wr, P)
+
+    def scan(out, a, b, o0, o1, R, Wr, P=()):
+        op("v", lambda e: e.tensor_tensor_scan(out, a, b, 0.0, o0, o1), R, Wr, P)
 
     def fill(x, c, key=None):
         op("v", lambda e: e.memset(x, c), (), [key or x.name])
@@ -176,7 +309,8 @@ def rank_program(g, core, T, topo):
     iota(T.kc[:, :], [[1, 32]], 0, 0, "kc")
     iota(T.KAP[:, :], [[113, 32]], 37, 0, "KAP")
     iota(T.K1c[:, :], [[-1, 32], [0, 8]], 32, 0, "K1c")
-    iota(T.K19[:, :], [[1, 32], [0, 8]], 0, 0, "K19")
+    iota(T.K19[:, :], [[-1, 32], [0, 8]], -1, 0, "K19")
+    iota(T.K18[:, :], [[-1, 32], [0, 8]], -1, 0, "K18")
     iota(T.K2c[:, :], [[-4096, 32], [0, 8]], 31 * 4096, 0, "K2c")
     iota(T.C32[:, :], [[16, 8]], 0, 0, "C32")
     fill(T.SEL[:, :], 0.0, "SELz")
@@ -187,6 +321,13 @@ def rank_program(g, core, T, topo):
     fill(T.SC0[:, :], -1000.0, "SC0z")
     fill(T.SC0[:, 0:128:16], 1000.0, "SC0z")
     fill(T.thr[:, :], 2.0, "thr")
+
+    for k, w in enumerate((-6.0, 2.0, 2.0, -2.0)):
+        act(T.IS[:, k * 128:k * 128 + 128], T.ID[:, :], ACT.Copy, ["ID"], ["IS%d" % k], scale=w)
+    for k in range(16):
+        x = slice(k * 128 + k, k * 128 + 128, 16)
+        act(T.SEL[:, x], T.G8[:, :], ACT.Copy, ["G8", "SELz"], ["SEL%d" % k])
+        act(T.SEL2[:, x], T.G8[:, :], ACT.Copy, ["G8", "SEL2z"], ["SEL2%d" % k], scale=131072.0)
 
     cp(T.pl0[:, 0:256], T.craw[:, :], ["ai"], ["plS"])
     ts(T.pl0[:, 256:512], T.cm[:, :], 2, A.add, R=["wi"], Wr=["plQ"])
@@ -201,27 +342,28 @@ def rank_program(g, core, T, topo):
         p = T["ps%d" % (c % 4)]
         bk = ["b%d" % (c % 4)]
         pk = ["rg%d" % (c % 4)]
+        scan(T.FL[:, x], T.EC[:, x], T.Gc[:, x], A.max, A.add, ["EC%d" % c, "Gc%d" % c], ["fx%d" % c])
         mm(p[:, :], T.ID[:, :], T.E[:, x], True, False, [e, "ID"], pk, bk)
-        mm(p[:, :], T.ID[:, :], T.Gc[:, x], False, False, ["Gc%d" % c], (), bk)
-        mm(p[:, :], T.ID[:, :], T.EC[:, x], False, True, ["EC%d" % c], pk, bk)
+        mm(p[:, :], T.ID[:, :], T.FL[:, x], False, True, ["fx%d" % c], pk, bk)
         act(T.TT[:, x], p[:, :], ACT.Copy, pk, ["TT%d" % c], bk)
     TK = ks("TT", 8)
-    for k in range(16):
-        cp(T.SEL[:, k * 128 + k:k * 128 + 128:16], T.G8[:, :], ["G8", "SELz"], ["SEL%d" % k])
     ts(T.ua[:, :], T.ui[:, :], 15, A.bitwise_and, R=["pi"], Wr=["pb"])
     tt(T.C32[:, :], T.C32[:, :], T.ua[:, :], A.add, ["C32", "pb"], ["C32"])
     ts(T.Cv[:, :], T.C32[:, :], 33.0, A.mult, 32.0, A.add, ["C32"], ["Cv"])
     ts(T.Cn[:, :], T.C32[:, :], 4096.0, A.add, R=["C32"], Wr=["Cn"])
     ts(T.C32[:, :], T.C32[:, :], 32.0, A.mult, R=["C32", "Cv", "Cn"], Wr=["C32"])
-    ts(T.K1c[:, :], T.K1c[:, :], 262144.0, A.mult, R=["K1c"], Wr=["K1c"])
+    ts(T.ps5[:, 128:384], T.K1c[:, :], 8192.0, A.mult, R=["K1c"], Wr=["K1c"], P=["b5"])
+    cp(T.ps6[:, 256:512], T.K2c[:, :], ["K2c"], ["K2c"], ["b6"])
+    fill(T.FOUR[:, :], 4.0, "FOUR")
+    for k, w in enumerate((0.5, 248.5, -7.5, -11.5, 5.0)):
+        fill(T.SG[:, k:k + 1], w, "sgn")
     ts(T.K19[:, :], T.K19[:, :], 524288.0, A.mult, R=["K19"], Wr=["K19"])
+    ts(T.K18[:, :], T.K18[:, :], 262144.0, A.mult, R=["K18"], Wr=["K18"])
     cp(T.barf[:, :], T.Mdi[:, :], ["bari"], ["barf"])
     for k in range(4):
         x = slice(k * 1024, k * 1024 + 1024)
         ts(T.ND[:, x], T.PT[:, x], 12.0, A.is_lt, R=["P%d" % k], Wr=["ND%d" % k])
     NK = ks("ND", 4)
-    for k in range(16):
-        ts(T.SEL2[:, k * 128 + k:k * 128 + 128:16], T.G8[:, :], 131072.0, A.mult, R=["G8", "SEL2z"], Wr=["SEL2%d" % k])
     tt(T.pp[:, 0:64], T.ID[:, 0:64], T.ID[:, 64:128], A.add, ["ID"], ["p1"])
     tt(T.pp[:, 128:160], T.pp[:, 0:32], T.pp[:, 32:64], A.add, ["p1"], ["p2"])
     tt(T.MK16[:, 0:16], T.pp[:, 128:144], T.pp[:, 144:160], A.add, ["p2"], ["MK16"])
@@ -229,34 +371,25 @@ def rank_program(g, core, T, topo):
     for t in range(VI):
         pl = T["pl%d" % t]
         last = t == VI - 1
-        PLK = ["plS", "plQ"]
         if t:
-            lands("ap%d" % t, len(topo.engines(T.cores[(rank - PLAN_GO) % N], core)), PLK)
+            n = len(topo.engines(T.cores[(rank - PLAN_GO) % N], core))
+            lands("ap%d" % t, n, ["plS"])
+            lands("aq%d" % t, n, ["plQ"])
             lands("as%d" % t, len(topo.engines(T.cores[(rank - STATE_GO) % N], core)), ["st"])
 
-        def ab(c):
-            for k in range(4 * c, 4 * c + 4):
-                src = T.Gc[:, k * 128:k * 128 + 128]
-                ts(T.D1[:, k + 1:33 * B:33], src, 12.0 + 4 * k, A.add, R=["Gc%d" % c], Wr=["D1%d" % k])
-                ts(T.D0[:, k + 1:33 * B:33], src, -16.0, A.mult, -6400.0, A.add, ["Gc%d" % c], ["D0%d" % k])
-
-        def vgc(c):
-            cp(T.Gc[:, c * 512:c * 512 + 512], T.TT[:, :].indirect(pl[:, c * 32:c * 32 + 32]), TK + ["plS"], ["Gc%d" % c])
-
-        for c in range(6):
-            act(T.Gc[:, c * 512:c * 512 + 512], T.TT[:, :].indirect(pl[:, c * 32:c * 32 + 32]), ACT.Copy, TK + ["plS"], ["Gc%d" % c])
+        for k in range(32 - NVG):
+            act(T.D1[:, k + 1:33 * B:33], T.TT[:, :].indirect(pl[:, k * 8:k * 8 + 8]), ACT.Identity, TK + ["plS"], ["D1%d" % k], bias=12.0 + 4 * k)
         for c in range(8):
-            act(T.Gn[:, c * 512:c * 512 + 512], T.ND[:, :].indirect(pl[:, c * 32:c * 32 + 32]), ACT.Identity, NK + ["plS"], ["Gn%d" % c],
-                scale=188.0, bias=4.0)
-        vgc(7)
+            out, src = T.Gn[:, c * 512:c * 512 + 512], T.ND[:, :].indirect(pl[:, c * 32:c * 32 + 32])
+            if c < NVD:
+                ts(out, src, 188.0, A.mult, 4.0, A.add, NK + ["plS"], ["Gn%d" % c])
+            else:
+                act(out, src, ACT.Identity, NK + ["plS"], ["Gn%d" % c], scale=188.0, bias=4.0)
+        for k in range(32 - NVG, 32):
+            ts(T.D1[:, k + 1:33 * B:33], T.TT[:, :].indirect(pl[:, k * 8:k * 8 + 8]), 12.0 + 4 * k, A.add, R=TK + ["plS"], Wr=["D1%d" % k])
         ts(T.D1[:, 0:33 * B:33], T["sc%d" % t][:, :], 4.0, A.add, R=["st"], Wr=["D1i"])
-        ab(7)
-        ab(0)
-        ab(1)
-        vgc(6)
-        ab(6)
-        for c in range(2, 6):
-            ab(c)
+        for k in range(32):
+            ts(T.D0[:, k + 1:33 * B:33], T.D1[:, k + 1:33 * B:33], -16.0, A.mult, -4960.0, A.add, ["D1%d" % k], ["D0%d" % k])
         op("v", lambda e: e.tensor_tensor_scan(T.V0[:, :], T.D0[:, :], T.D1[:, :], 0.0, A.min, A.max),
            ks("D0", 32) + ks("D1", 32) + ["D0i", "D1i"], ["V0"])
         if t:
@@ -282,18 +415,19 @@ def rank_program(g, core, T, topo):
 
         for c in range(4):
             ndps(c)
-        ts(T.t64[:, :], pl[:, :], 64.0, A.mult, R=PLK, Wr=["t64"])
-        tt(T.ps6[:, 0:256], T.t64[:, 0:256], T.K1c[:, :], A.add, ["t64", "K1c"], ["K1"], ["b6"])
         flaw(0)
         ndps(4)
         flaw(1)
-        count(T.FL, "FL", "SEL", T.ps4, "b4", 0, "CN")
         ndps(5)
+        if EARLY:
+            count(T.FL, "FL", "SEL", T.ps4, "b4", 0, "CN")
         flaw(2)
         ndps(6)
         flaw(3)
-        count(T.FL, "FL", "SEL", T.ps4, "b4", 1, "CN")
         ndps(7)
+        if not EARLY:
+            count(T.FL, "FL", "SEL", T.ps4, "b4", 0, "CN")
+        count(T.FL, "FL", "SEL", T.ps4, "b4", 1, "CN")
         for c in (4, 5):
             flaw(c)
         count(T.FL, "FL", "SEL", T.ps4, "b4", 2, "CN")
@@ -302,22 +436,25 @@ def rank_program(g, core, T, topo):
         count(T.FL, "FL", "SEL", T.ps4, "b4", 3, "CN")
 
         v32 = T.V0[:, 32:33 * B:33]
-        for k, (cut, o, s) in enumerate(((0.0, A.is_lt, 12.0), (-248.0, A.is_lt, -4.0), (8.0, A.is_ge, 4.0), (12.0, A.is_ge, -4.0))):
-            ts(T.pp[:, k * 128:k * 128 + 128], v32, cut, o, s, A.mult, ["V0"], ["p%d" % (k + 1)])
-        for k in range(4):
-            mm(T.ps5[:, 256:384], T.ID[:, :], T.pp[:, k * 128:k * 128 + 128], k == 0, k == 3, ["ID", "p%d" % (k + 1)], ["SP"] if k in (0, 3) else (), ["b5"])
+        for k, cut in enumerate((0.5, 248.5, -7.5, -11.5)):
+            act(T.pp[:, k * 128:k * 128 + 128], v32, ACT.Sign, ["V0", "sgn"], ["p%d" % (k + 1)], bias=T.SG[:, k:k + 1])
+        cp(T.K2[:, :], pl[:, 0:256], ["plS"], ["Sf"])
+        act(T.t64S[:, :], T.K2[:, :], ACT.Copy, ["Sf"], ["t64S"], scale=64.0)
+        tt(T.ps6[:, 0:256], T.K2[:, :], T.ps5[:, 128:384], A.add, ["Sf", "K1c"], ["K1"], ["b6", "b5"])
+        for k in range(5):
+            mm(T.ps5[:, 384:512], T.IS[:, (k % 4) * 128:(k % 4) * 128 + 128] if k < 4 else T.ID[:, :], T.pp[:, k * 128:k * 128 + 128] if k < 4 else T.FOUR[:, :],
+               k == 0, k == 4, ["IS%d" % (k % 4), "ID", "FOUR", "p%d" % (k % 4 + 1)], ["SP"] if k in (0, 4) else (), ["b5"])
         cp(T.vi[:, :], v32, ["V0"], ["vi"])
         ts(T.e2[:, :], T.vi[:, :], 3, A.bitwise_and, R=["vi"], Wr=["e2"])
 
         ts(T.o1[:, :], T.ps4[:, 0:256], T.thr[:, :], A.is_ge, R=ks("CN", 4) + ["thr"], Wr=["o1"], P=["b4"])
         tt(T.prod1[:, :], T.o1[:, :], T.ps6[:, 0:256], A.mult, ["o1", "K1"], ["prod1"], ["b6"])
-        gred(T.M8, T.prod1, A.max, ["prod1"], "M8")
-        cp(T.M8i[:, :], T.M8[:, :], ks("M8", 8), ["M8i"])
-        ts(T.xr[:, :], T.M8i[:, :], 18, A.arith_shift_right, R=["M8i"], Wr=["xr"])
-        ts(T.sx[:, :], T.M8i[:, :], 6, A.arith_shift_right, 4095, A.bitwise_and, ["M8i"], ["sx"])
-        ts(T.n16[:, 0:8], T.xr[:, :], -128.0, A.mult, R=["xr"], Wr=["xm"])
+        gred(T.M8i, T.prod1, A.max, ["prod1"], "M8")
+        ts(T.xr[:, :], T.M8i[:, :], 13, A.arith_shift_right, R=ks("M8", 8), Wr=["xr"])
+        ts(T.sx[:, :], T.M8i[:, :], 4095, A.bitwise_and, R=ks("M8", 8), Wr=["sx"])
+        ts(T.xm[:, :], T.M8i[:, :], 6, A.arith_shift_right, 0x7FF80, A.bitwise_and, ks("M8", 8), ["xm"])
         tt(T.oi[:, 0:8], T.Cv[:, :], T.xr[:, :], A.subtract, ["Cv", "xr"], ["oi0"])
-        tt(T.oi[:, 8:16], T.Cn[:, :], T.n16[:, 0:8], A.add, ["Cn", "xm"], ["oi1"])
+        tt(T.oi[:, 8:16], T.Cn[:, :], T.xm[:, :], A.subtract, ["Cn", "xm"], ["oi1"])
         cp(T.ou[:, :], T.oi[:, :], ["oi0", "oi1"], ["ou"])
         GNK = ks("Gn", 8) + ["Gnx"]
         act(T.vx[:, :], T.V0[:, :].indirect(T.ou[:, 0:8]), ACT.Copy, ["V0", "ou"], ["vx"])
@@ -326,36 +463,43 @@ def rank_program(g, core, T, topo):
         mm(T.ps7[:, 0:128], T.y[:, :], T.ID[:, :], True, True, ["y", "ID"], ["DT"], ["b7"])
         tt(T.W4[:, 0:128], T.Gn[:, :].indirect(T.ou[:, 8:16]), T.t12[:, :], A.max, GNK + ["ou", "t12"], ["W4a"])
         op("v", lambda e: e.tensor_tensor_scan(T.RM[:, :], T.SC0[:, :], T.ps7[:, 0:128], 0.0, A.max, A.min), ["SC0z", "DT"], ["RM"], ["b7"])
+        ts(T.xf[:, :], T.xr[:, :], -1.0, A.mult, 32.0, A.add, ["xr"], ["xf"])
         for h in range(8):
-            ts(T.LT[:, h * 16:h * 16 + 16], T.MK16[:, 0:16], T.RM[:, h * 16 + 15:h * 16 + 16], A.mult, R=["MK16", "RM"], Wr=["LT%d" % h])
+            out, col = T.LT[:, h * 16:h * 16 + 16], T.RM[:, h * 16 + 15:h * 16 + 16]
+            if h < 5:
+                ts(out, T.MK16[:, 0:16], col, A.mult, R=["MK16", "RM"], Wr=["LT%d" % h])
+            else:
+                act(out, T.MK16[:, 0:16], ACT.Identity, ["MK16", "RM"], ["LT%d" % h], scale=col)
         mm(T.ps7[:, 256:264], T.LT[:, :], T.G8[:, :], True, True, ks("LT", 8) + ["G8"], ["D8"], ["b7"])
         for k in range(4):
             mm(T.ps0[:, k * 128:k * 128 + 128], T.ID[:, :], T.W4[:, 0:128], True, True, ["ID", "W4a"], ["rg0"], ["b0"])
-        ts(T.xf[:, :], T.xr[:, :], -1.0, A.mult, 32.0, A.add, ["xr"], ["xf"])
-        ts(T.di[:, :], T.ps7[:, 256:264], -1.0, A.mult, -8.0, A.add, ["D8"], ["di"], ["b7"])
-        ts(T.dg[:, :], T.di[:, :], 2, A.arith_shift_right, 63, A.bitwise_and, ["di"], ["dg"])
-        tt(T.d8[:, :], T.dg[:, :], T.xf[:, :], A.min, ["dg", "xf"], ["d8"])
-        for h in range(8):
-            ts(T.eq[:, h:256:8], T.kc[:, :], T.d8[:, h:h + 1], A.is_equal, R=["kc", "d8"], Wr=["eq%d" % h])
-        tt(T.prod1[:, :], T.eq[:, :], T.ps6[:, 0:256], A.mult, ks("eq", 8) + ["K1"], ["prod1"], ["b6"])
-        gred(T.M8, T.prod1, A.max, ["prod1"], "M8")
-        cp(T.Mdi[:, :], T.M8[:, :], ks("M8", 8), ["Mdi"])
-        ts(T.sd[:, :], T.Mdi[:, :], 6, A.arith_shift_right, 4095, A.bitwise_and, ["Mdi"], ["sd"])
-        tt(T.pr0[:, :], T.sx[:, :], T.sd[:, :], A.mult, ["sx", "sd"], ["pr0"])
+        ts(T.ncd[:, :], T.xr[:, :], -8192.0, A.mult, 262144.0, A.add, ["xr"], ["xs"])
+        ts(T.di[:, :], T.ps7[:, 256:264], -2048.0, A.mult, -16384.0, A.add, ["D8"], ["di"], ["b7"])
+        ts(T.dg[:, :], T.di[:, :], 63 << 13, A.bitwise_and, R=["di"], Wr=["dg"])
+        tt(T.d8[:, :], T.dg[:, :], T.ncd[:, :], A.min, ["dg", "xs"], ["d8"])
         cp(T.sxf[:, :], T.sx[:, :], ["sx"], ["sxf"])
-        if t:
-            ts(T.pr0[:, :], T.pr0[:, :], 32.0 * 97 * t, A.add, R=["pr0"], Wr=["pr0"])
+        for h in range(8):
+            ts(T.prod1[:, h:256:8], T.ps6[:, h:256:8], -262144.0, A.add, T.d8[:, h:h + 1], A.add, ["K1", "d8"], ["df%d" % h], ["b6"])
+        for h in range(8):
+            op("v", lambda e, h=h: e.tensor_reduce(T.sd[:, h:h + 1], T.prod1[:, h:256:8], AX, A.min, apply_absolute_value=True), ["df%d" % h], ["sd%d" % h])
+        SD = ks("sd", 8)
+        for k in range(2):
+            act(T.base24[:, k * 8:k * 8 + 8], T.xf[:, :], ACT.Copy, ["xf"], ["ba%d" % k])
+        act(T.c16[:, 8:16], T.xf[:, :], ACT.Copy, ["xf"], ["c161"])
+        act(T.m24[:, 0:8], T.xf[:, :], ACT.Copy, ["xf"], ["m240"], scale=-1.0, bias=99.0)
+        act(T.Mb[:, :], T.W4[:, 0:128], ACT.Relu, ["W4a", "sgn"], ["Mb"], scale=-1.0, bias=T.SG[:, 4:5])
+        for k in range(1, 4):
+            act(T.W4[:, k * 128:k * 128 + 128], T.W4[:, 0:128], ACT.Copy, ["W4a"], ["W4%d" % k])
+        tt(T.pr0[:, :], T.sx[:, :], T.sd[:, :], A.mult, ["sx"] + SD, ["pr0"])
         ts(T.bs[:, :], T.pr0[:, :], 5, A.arith_shift_right, R=["pr0"], Wr=["bs"])
-        cp(T.bsf[:, :], T.bs[:, :], ["bs"], ["bsf"])
+        ts(T.bsf[:, :], T.bs[:, :], 97.0 * t, A.add, R=["bs"], Wr=["bsf"])
         for h in range(8):
             ts(T.craw[:, h:256:8], T.KAP[:, :], T.sxf[:, h:h + 1], A.mult, T.bsf[:, h:h + 1], A.add, ["KAP", "sxf", "bsf"], ["craw%d" % h])
         ts(T.cm[:, :], T.craw[:, :], 4095, A.bitwise_and, R=ks("craw", 8), Wr=["cm"])
         cp(T.cu[:, :], T.cm[:, :], ["cm"], ["cu"])
 
-        for c in range(6):
+        for c in range(NSC):
             act(T.EC[:, c * 512:c * 512 + 512], T.E[:, :].indirect(T.cu[:, c * 32:c * 32 + 32]), ACT.Copy, EK + ["cu"], ["EC%d" % c])
-        for k in range(1, 4):
-            cp(T.W4[:, k * 128:k * 128 + 128], T.W4[:, 0:128], ["W4a"], ["W4%d" % k])
 
         def vfuse(c):
             tt(T.FL[:, c * 512:c * 512 + 512], T.E[:, :].indirect(T.cu[:, c * 32:c * 32 + 32]), T.W4[:, :], A.is_ge,
@@ -368,8 +512,7 @@ def rank_program(g, core, T, topo):
             count(T.FL, "FL", "SEL2", T.ps4, "b4", c, "CN")
 
         vfuse(7)
-        tt(T.sv[:, :], T.e2[:, :], T.ps5[:, 256:384], A.add, ["e2", "SP"], ["sv"], ["b5"])
-        ts(T.Mb[:, :], T.W4[:, 0:128], 4.0, A.is_equal, R=["W4a"], Wr=["Mb"])
+        tt(T.sv[:, :], T.e2[:, :], T.ps5[:, 384:512], A.add, ["e2", "SP"], ["sv"], ["b5"])
         hit(0)
         for k in range(16):
             mm(T.ps7[:, 272:280], T.SEL[:, k * 128:k * 128 + 128], T.sv[:, k:128:16], k == 0, k == 15, ["sv", "SEL%d" % k], ["U8"] if k in (0, 15) else (), ["b7"])
@@ -380,24 +523,22 @@ def rank_program(g, core, T, topo):
             ts(T.sq[:, :], T.sv[:, :], 8.0, A.is_ge, -264.0, A.mult, ["sv"], ["sq"])
             tt(so[:, :], T.sv[:, :], T.sq[:, :], A.add, ["sv", "sq"], ["so"])
             dst = T.cores[(rank + STATE_GO) % N]
-            rid, pid, _ = topo.addr(dst)
             n = len(topo.engines(core, dst))
-            send(lambda: g.remote_dma(T["sc%d" % (t + 1)][:, :], so[:, :], T.sem["as%d" % (t + 1)], T.sem["ls%d" % (t + 1)], pid, rid, topo.mask(core, dst)),
-                 ["so"], "ls%d" % (t + 1), n)
+            send(remote(T["sc%d" % (t + 1)][:, :], so[:, :], "as%d" % (t + 1), "ls%d" % (t + 1), dst), ["so"], "ls%d" % (t + 1), n)
         hit(1)
         score(0)
-        vfuse(6)
-        score(3)
-        tt(T.K2[:, :], T.K2c[:, :], T.cm[:, :], A.add, ["K2c", "cm"], ["K2"])
+        if NSC == 6:
+            vfuse(6)
+            score(3)
+        tt(T.K2[:, :], T.cm[:, :], T.ps6[:, 256:512], A.add, ["K2c", "cm"], ["K2"], ["b6"])
         hit(2)
-        for k in range(2):
-            cp(T.base24[:, k * 8:k * 8 + 8], T.xf[:, :], ["xf"], ["ba%d" % k])
         if t == 0:
             fill(T.base24[:, 16:24], 0.0, "ba2")
-        ts(T.m24[:, 0:8], T.xf[:, :], -1.0, A.mult, 99.0, A.add, ["xf"], ["m240"])
-        tt(T.m24[:, 8:16], T.d8[:, :], T.xf[:, :], A.subtract, ["d8", "xf"], ["m241"])
-        ts(T.m24[:, 16:24], T.sd[:, :], 64.0, A.mult, 128.0, A.add, ["sd"], ["m242"])
-        ts(T.fnd[:, :], T.xr[:, :], 1.0, A.is_ge, R=["xr"], Wr=["fnd"])
+        tt(T.aqt[:, :], T.d8[:, :], T.ncd[:, :], A.subtract, ["d8", "xs"], ["dxs"])
+        ts(T.m24[:, 8:16], T.aqt[:, :], 1.0 / 8192, A.mult, R=["dxs"], Wr=["m241"])
+        ts(T.cm64[:, :], T.cm[:, :], 64.0, A.mult, -16777216.0, A.add, ["cm"], ["cm64"])
+        ts(T.m24[:, 16:24], T.sd[:, :], 64.0, A.mult, 128.0, A.add, SD, ["m242"])
+        ts(T.fnd[:, :], T.xr[:, :], 1.0, A.is_ge, 131072.0, A.mult, ["xr"], ["fnd"])
         tt(T.barM[:, :], T.barf[:, :], T.ps5[:, 0:8], A.add, ["barf", "NM"], ["barM"], ["b5"])
         hit(3)
         score(1)
@@ -410,6 +551,10 @@ def rank_program(g, core, T, topo):
         cp(T.uu[:, :], T.uo[:, :], ["uo"], ["uu"])
         hit(5)
         score(2)
+        ts(T.t64[:, :], pl[:, 256:512], 64.0, A.mult, R=["plQ"], Wr=["t64Q"])
+        if NSC == 7:
+            hit(6)
+            score(3)
         tt(T.es[:, :], T.E[:, :].indirect(T.uu[:, :]), T.sv[:, :], A.add, EK + ["uu", "sv"], ["es"])
         ts(T.en[:, :], T.es[:, :], 1, A.arith_shift_right, R=["es"], Wr=["en"])
         cp(T.eb[:, :], T.en[:, :], ["en"], ["eb"])
@@ -418,20 +563,21 @@ def rank_program(g, core, T, topo):
             op("y", lambda e: e.dma_start(T.ye[:, :], T.E[:, :]), EK, ["ye"], (), "ds0", 16)
 
         tt(T.key2[:, :], T.K2[:, :], T.ps4[:, 0:256], A.add, ["K2"] + ks("CN", 4), ["key2"], ["b4"])
-        gred(T.M8, T.key2, A.max, ["key2"], "M8")
-        cp(T.MBi[:, :], T.M8[:, :], ks("M8", 8), ["MBi"])
+        gred(T.MBi, T.key2, A.max, ["key2"], "MBi")
+        MB = ks("MBi", 8)
         for k in range(3):
-            op("v", lambda e, k=k: e.tensor_scalar(T.oi24[:, k * 8:k * 8 + 8], T.MBi[:, :], 17, None, A.arith_shift_right), ["MBi"], ["bt%d" % k])
-        ts(T.cb[:, :], T.MBi[:, :], 4095, A.bitwise_and, R=["MBi"], Wr=["cb"])
-        tt(T.ret24[:, :], T.oi24[:, :], T.bar24[:, :], A.is_lt, ks("bt", 3) + ks("br", 3), ["ret"])
-        tt(T.pr24[:, :], T.ret24[:, :], T.m24[:, :], A.mult, ["ret"] + ks("m24", 3), ["pr24"])
+            tt(T.ret24[:, k * 8:k * 8 + 8], T.MBi[:, :], T.bar24[:, k * 8:k * 8 + 8], A.is_lt, MB + ["br%d" % k], ["ret%d" % k])
+        tt(T.pr24[:, :], T.ret24[:, :], T.m24[:, :], A.mult, ks("ret", 3) + ks("m24", 3), ["pr24"])
+        ts(T.cb[:, :], T.MBi[:, :], 4095, A.bitwise_and, R=MB, Wr=["cb"])
+        ts(T.cbx[:, :], T.cb[:, :], 64.0, A.mult, -16777216.0, A.add, ["cb"], ["cbx"])
+        ts(T.nr[:, :], T.ret24[:, 0:8], -1.0, A.mult, 1.0, A.add, ["ret0"], ["nr"])
         tt(T.a24[:, :], T.base24[:, :], T.pr24[:, :], A.add, ["pr24"] + ks("ba", 3), ["a24"])
         for h in range(8):
             ts(T.ps0[:, h:256:8], T.kc[:, :], T.a24[:, h:h + 1], A.min, T.a24[:, 8 + h:9 + h], A.not_equal, ["kc", "a24"], ["e1%d" % h], ["b0"])
-            ts(T.e2p[:, h:256:8], T.t64[:, 256 + h:512:8], T.a24[:, 16 + h:17 + h], A.not_equal, R=["t64", "a24"], Wr=["e2p%d" % h])
-        tt(T.kept[:, :], T.e2p[:, :], T.ps0[:, 0:256], A.min, ks("e1", 8) + ks("e2p", 8), ["kept"], ["b0"])
+            ts(T.o1[:, h:256:8], T.t64[:, h:256:8], T.a24[:, 16 + h:17 + h], A.not_equal, R=["t64Q", "a24"], Wr=["e2p%d" % h])
+        tt(T.kept[:, :], T.o1[:, :], T.ps0[:, 0:256], A.min, ks("e1", 8) + ks("e2p", 8), ["kept"], ["b0"])
         if not last:
-            cp(T.retb[:, :], T.ret24[:, 0:8], ["ret"], ["retb"])
+            cp(T.retb[:, :], T.ret24[:, 0:8], ["ret0"], ["retb"])
             mm(T.ps7[:, 280:288], T.ONE[:, :], T.retb[:, :], True, True, ["ONE", "retb"], ["RS"], ["b7"])
         for h in range(8):
             op("v", lambda e, h=h: e.tensor_tensor_scan(T.ps1[:, h:256:8], T.ONES32[:, :], T.kept[:, h:256:8], 1.0, A.add, A.subtract),
@@ -440,60 +586,80 @@ def rank_program(g, core, T, topo):
         op("v", lambda e: e.memset(T.ZS[:, 0:8], 0), (), ["ZS0"])
         op("v", lambda e: e.memset(T.ZQ[:, 0:8], 0), (), ["ZQ0"])
         tt(T.ps0[:, 256:512], T.K19[:, :], T.ps1[:, 256:512], A.add, ["K19", "shk"], ["ksh"], ["b0", "b1"])
-        tt(T.ZS[:, 8:264], T.t64[:, 0:256], T.ps0[:, 256:512], A.add, ["t64", "ksh"], ["ZS"], ["b0"])
-        tt(T.ZQ[:, 8:264], T.t64[:, 256:512], T.ps0[:, 256:512], A.add, ["t64", "ksh"], ["ZQ"], ["b0"])
+        tt(T.key2[:, :], T.K18[:, :], T.ps1[:, 256:512], A.add, ["K18", "shk"], ["kss"], ["b1"])
+        tt(T.ZS[:, 8:264], T.t64S[:, :], T.key2[:, :], A.add, ["t64S", "kss"], ["ZS"])
+        tt(T.ZQ[:, 8:264], T.t64[:, :], T.ps0[:, 256:512], A.add, ["t64Q", "ksh"], ["ZQ"], ["b0"])
         for k in range(2):
-            ts(T.n16[:, k * 8:k * 8 + 8], T.ps1[:, 248:256], -1.0, A.mult, 33.0, A.add, ks("sp", 8), ["n16%d" % k, "xm"], ["b1"])
+            ts(T.n16[:, k * 8:k * 8 + 8], T.ps1[:, 248:256], -1.0, A.mult, 33.0, A.add, ks("sp", 8), ["n16%d" % k], ["b1"])
         if t == 0:
             fill(T.c16[:, 0:8], 99.0, "c160")
-        cp(T.c16[:, 8:16], T.xf[:, :], ["xf"], ["c161"])
-        ts(T.nr[:, :], T.ret24[:, 0:8], -1.0, A.mult, 1.0, A.add, ["ret"], ["nr"])
-        ts(T.aqt[:, :], T.sd[:, :], 1.0, A.add, R=["sd"], Wr=["aqt"])
+        ts(T.aqt[:, :], T.sd[:, :], 1.0, A.add, R=SD, Wr=["aqt"])
         tt(T.d16[:, :], T.n16[:, :], T.c16[:, :], A.subtract, ["n160", "n161", "c160", "c161"], ["d16"])
-        tt(T.cbr[:, :], T.cb[:, :], T.nr[:, :], A.mult, ["cb", "nr"], ["cbr"])
+        tt(T.cbr[:, :], T.cbx[:, :], T.nr[:, :], A.mult, ["cbx", "nr"], ["cbr"])
         tt(T.aq[:, :], T.aqt[:, :], T.nr[:, :], A.mult, ["aqt", "nr"], ["aq0"])
-        tt(T.r16[:, :], T.d16[:, :], T.ret24[:, 0:16], A.mult, ["d16", "ret"], ["r16"])
+        tt(T.r16[:, :], T.d16[:, :], T.ret24[:, 0:16], A.mult, ["d16", "ret0", "ret1"], ["r16"])
         ts(T.aq[:, :], T.aq[:, :], 1.0, A.add, R=["aq0"], Wr=["aq"])
         tt(T.f16[:, :], T.r16[:, :], T.c16[:, :], A.add, ["r16", "c160", "c161"], ["f16"])
         for h in range(8):
-            ts(T.ps1[:, h:256:8], T.cm[:, h:256:8], T.ret24[:, h:h + 1], A.mult, T.cbr[:, h:h + 1], A.add, ["cm", "ret", "cbr"], ["al%d" % h, "sp%d" % h], ["b1"])
+            act(T.K2[:, h:256:8], T.cm64[:, h:256:8], ACT.Identity, ["cm64", "ret0", "cbr"], ["al%d" % h], scale=T.ret24[:, h:h + 1], bias=T.cbr[:, h:h + 1])
         for h in range(8):
-            ts(T.ps0[:, h:256:8], T.kc[:, :], T.f16[:, h:h + 1], A.min, T.f16[:, 8 + h:9 + h], A.is_equal, ["kc", "f16"], ["Fp%d" % h, "e1%d" % h], ["b0"])
+            ts(T.ps0[:, h:256:8], T.kc[:, :], T.f16[:, h:h + 1], A.min, T.f16[:, 8 + h:9 + h], A.is_equal, ["kc", "f16"], ["Fp%d" % h], ["b0"])
+        tt(T.ps1[:, 0:256], T.K2[:, :], T.ps0[:, 0:256], A.mult, ks("al", 8) + ks("Fp", 8), ["alY"], ["b0", "b1"])
         for b in range(6):
             s = 1 << b
             m = (33 - s) * 8
             z = ["ZS", "ZS0"]
             q = ["ZQ", "ZQ0"]
-            ts(T.tb[:, 0:m], T.ZS[:, 8 * s:264], b, A.arith_shift_right, 1, A.bitwise_and, z, ["tb"])
-            tt(T.ps3[:, 0:m], T.tb[:, 0:m], T.ZQ[:, 8 * s:264], A.mult, ["tb"] + q, ["mvQ"], ["b3"])
-            tt(T.ps2[:, 0:m], T.tb[:, 0:m], T.ZS[:, 8 * s:264], A.mult, ["tb"] + z, ["mvS"], ["b2"])
-            tt(T.ZQ[:, 0:m], T.ZQ[:, 0:m], T.ps3[:, 0:m], A.max, q + ["mvQ"], q, ["b3"])
-            tt(T.ZS[:, 0:m], T.ZS[:, 0:m], T.ps2[:, 0:m], A.max, z + ["mvS"], z, ["b2"])
-        ts(T.nQ[:, :], T.ZQ[:, 0:256], 6, A.arith_shift_right, 8191, A.bitwise_and, ["ZQ", "ZQ0"], ["nQ"])
-        ts(T.nS[:, :], T.ZS[:, 0:256], 6, A.arith_shift_right, 8191, A.bitwise_and, ["ZS", "ZS0"], ["nS"])
-        for h in range(8):
-            ts(T.dfQ[:, h:256:8], T.nQ[:, h:256:8], -1.0, A.mult, T.aq[:, h:h + 1], A.add, ["nQ", "aq"], ["dfQ%d" % h])
-        tt(T.dfS[:, :], T.ps1[:, 0:256], T.nS[:, :], A.subtract, ks("al", 8) + ["nS"], ["dfS"], ["b1"])
-        tt(T.ps3[:, 0:256], T.dfQ[:, :], T.ps0[:, 0:256], A.mult, ks("dfQ", 8) + ks("Fp", 8), ["mvQ"], ["b3", "b0"])
-        tt(T.ps2[:, 0:256], T.dfS[:, :], T.ps0[:, 0:256], A.mult, ["dfS"] + ks("Fp", 8), ["mvS"], ["b2", "b0"])
+            tb = T.tb[:, b * 264:b * 264 + m]
+            ts(tb, T.ZS[:, 8 * s:264], b, A.arith_shift_right, 1, A.bitwise_and, z, ["tb%d" % b])
+            scan(T.ps2[:, 0:m], tb, T.ZS[:, 8 * s:264], A.max, A.mult, ["tb%d" % b] + z, ["mvS"], ["b2"])
+            scan(T.ps3[:, 0:m], tb, T.ZQ[:, 8 * s:264], A.max, A.mult, ["tb%d" % b] + q, ["mvQ"], ["b3"])
+            tt(T.ZS[:, 0:m], T.ZS[:, 0:m], T.ps2[:, 0:m], A.min, z + ["mvS"], z, ["b2"])
+            tt(T.ZQ[:, 0:m], T.ZQ[:, 0:m], T.ps3[:, 0:m], A.min, q + ["mvQ"], q, ["b3"])
+        tt(T.ZS[:, 0:256], T.ZS[:, 0:256], T.ps1[:, 0:256], A.min, z + ["alY"], z, ["b1"])
+        ts(T.nS[:, :], T.ZS[:, 0:256], 6, A.arith_shift_right, 4095, A.bitwise_and, ["ZS", "ZS0"], ["nS"])
+
+        def reasons():
+            ts(T.nQ[:, :], T.ZQ[:, 0:256], 6, A.arith_shift_right, 8191, A.bitwise_and, ["ZQ", "ZQ0"], ["nQ"])
+            for h in range(8):
+                ts(T.prod1[:, h:256:8], T.nQ[:, h:256:8], -1.0, A.mult, T.aq[:, h:h + 1], A.add, ["nQ", "aq"], ["dfQ%d" % h])
+            tt(T.ps3[:, 0:256], T.prod1[:, :], T.ps0[:, 0:256], A.mult, ks("dfQ", 8) + ks("Fp", 8), ["mvQ"], ["b3", "b0"])
+
         if not last:
-            tt(T.fin[:, 256:512], T.nQ[:, :], T.ps3[:, 0:256], A.add, ["nQ", "mvQ"], ["finQ"], ["b3"])
-            tt(T.fin[:, 0:256], T.nS[:, :], T.ps2[:, 0:256], A.add, ["nS", "mvS"], ["finS"], ["b2"])
             po = T["plo%d" % t]
-            cp(po[:, :], T.fin[:, :], ["finS", "finQ"], ["po"])
             dst = T.cores[(rank + PLAN_GO) % N]
-            rid, pid, _ = topo.addr(dst)
             n = len(topo.engines(core, dst))
-            send(lambda: g.remote_dma(T["pl%d" % (t + 1)][:, :], po[:, :], T.sem["ap%d" % (t + 1)], T.sem["lp%d" % (t + 1)], pid, rid, topo.mask(core, dst)),
-                 ["po"], "lp%d" % (t + 1), n)
+
+            def go(half, s):
+                x = slice(half * 256, half * 256 + 256)
+                cp(po[:, x], (T.nS, T.nQ)[half][:, :], [("nS", "nQ")[half]], ["po%d" % half])
+                send(remote(T["pl%d" % (t + 1)][:, x], po[:, x], "a%s%d" % (s, t + 1), "l%s%d" % (s, t + 1), dst), ["po%d" % half],
+                     "l%s%d" % (s, t + 1), n)
+
+            go(0, "p")
             ts(T.pp[:, 0:128], T.eb[:, :], 4.0, A.is_ge, -520.0, A.mult, ["eb"], ["p1"])
             ts(T.pp[:, 128:256], T.eb[:, :], 12.0, A.is_ge, 252.0, A.mult, ["eb"], ["p2"])
             tt(T.pp[:, 256:384], T.pp[:, 0:128], T.pp[:, 128:256], A.add, ["p1", "p2"], ["p3"])
             tt(T.TT[:, :].indirect(T.uu[:, :]), T.eb[:, :], T.pp[:, 256:384], A.add, ["eb", "p3", "uu"], TK)
+            reasons()
+            tt(T.nQ[:, :], T.nQ[:, :], T.ps3[:, 0:256], A.add, ["nQ", "mvQ"], ["nQ"], ["b3"])
+            go(1, "q")
         else:
-            tt(T.ysw[:, 0:256], T.nS[:, :], T.ps2[:, 0:256], A.add, ["nS", "mvS"], ["ysw0"], ["b2"])
+            cp(T.ysw[:, 0:256], T.nS[:, :], ["nS"], ["ysw0"])
             op("y", lambda e: e.dma_start(T.ys[:, :], T.ysw[:, 0:256]), ["ysw0"], ["ys"], (), "ds1", 16)
-            tt(T.dfQ[:, :], T.nQ[:, :], T.ps3[:, 0:256], A.add, ["nQ", "mvQ"] + ks("dfQ", 8), ["dfQ"], ["b3"])
-            ts(T.ysw[:, 256:512], T.dfQ[:, :], 2.0, A.subtract, R=["dfQ"], Wr=["ysw1"])
+            reasons()
+            tt(T.K2[:, :], T.nQ[:, :], T.ps3[:, 0:256], A.add, ["nQ", "mvQ"], ["dfS"], ["b3"])
+            ts(T.ysw[:, 256:512], T.K2[:, :], 2.0, A.subtract, R=["dfS"], Wr=["ysw1"])
             op("s", lambda e: e.dma_start(T.yw[:, :], T.ysw[:, 256:512]), ["ysw1"], ["yw"], (), "ds2", 16)
+    order, deps = _schedule(prog)
+    tok = {}
+    for i in order:
+        kind, q, fn, R, Wr, P, sem, inc = prog[i]
+        toks = [tok[j] for j in sorted(deps[i]) if not (q == "t" and prog[j][1] == "t")]
+        if kind == "op":
+            tok[i] = op_now(q, fn, toks, P, sem, inc)
+        elif kind == "send":
+            tok[i] = send_now(fn, toks, inc[0], inc[1])
+        else:
+            tok[i] = lands_now(inc[0], inc[1])
     finish()

from concourse.mybir import AluOpType, AxisListType, ActivationFunctionType

A = AluOpType
ACT = ActivationFunctionType
AX = AxisListType.X
W, L, B, VI = 4096, 32, 128, 3
PLAN_GO, STATE_GO = 3, 1
H, F, I, U = "bfloat16", "float32", "int32", "uint16"

SCRATCH = {}


def _buf(dtype, n, *names):
    for x in names:
        SCRATCH[x] = ("sbuf", [128, n], dtype)


_buf(H, W, "E", "PT", "TT", "ND", "Gc", "FL", "EC")
_buf(H, 33 * B, "Gn", "D0", "D1", "V0")
_buf(H, 2048, "SEL", "SEL2")
_buf(H, 128, "ID", "ONE", "MK16", "SC0", "FOUR", "LT", "vx", "t12", "y", "Mb", "sv", "sq", "eb", "sc0", "sc1", "sc2", "so0", "so1")
_buf(H, 8, "G8", "retb")
_buf(H, 32, "ONES32")
_buf(H, 512, "W4", "pp", "IS")
_buf(F, 128, "RM")
_buf(H, 256, "o1", "kept")
_buf(F, 256, "K1c", "K19", "K18", "K2c", "K2", "prod1", "key2", "cm64", "t64", "t64S")
_buf(F, 32, "kc", "KAP")
_buf(F, 512, "ysw")
_buf(F, 8, "Cv", "Cn", "C32", "SG", "ncd", "xf", "d8", "sxf", "bsf", "barf", "barM", "fnd", "nr", "cbx", "cbr", "aq", "aqt")
_buf(F, 24, "base24", "m24", "best24", "bar24", "ret24", "pr24", "a24")
_buf(F, 16, "n16", "c16", "d16", "r16", "f16")
_buf(F, 1, "rs", "thr")
_buf(I, 2, "ri")
_buf(I, 6 * 264, "tb")
_buf(I, 256, "craw", "cm")
_buf(I, 8, "M8i", "xr", "xm", "sx", "di", "dg", "Mdi", "sd", "pr0", "bs", "MBi", "cb", "ui", "ua", "uo")
_buf(I, 16, "oi")
_buf(I, 128, "vi", "e2", "es", "en")
_buf(I, 264, "ZS", "ZQ")
_buf(I, 256, "nS", "nQ")
_buf(U, 512, "pl0", "pl1", "pl2", "plo0", "plo1")
_buf(U, 256, "cu")
_buf(U, 16, "ou")
_buf(U, 8, "uu")
for _b in range(8):
    SCRATCH["ps%d" % _b] = ("psum", [128, 512], F)

DMAS = ["ld%d" % k for k in range(12)] + ["ds%d" % k for k in range(3)]
SEMAPHORES = ["qv", "qs", "qt", "qg"] + DMAS + ["ap1", "ap2", "aq1", "aq2", "as1", "as2", "lp1", "lp2", "lq1", "lq2", "ls1", "ls2"]
NSC = 6
EARLY = True
NVD = 1
NVG = 14


def _tracker(g, T):
    eng = {"v": g.vector, "s": g.scalar, "t": g.tensor, "g": g, "y": g.sync}
    cnt, bank = {}, {}
    known = {q: {} for q in eng}

    def settle(q, toks):
        best = {}
        for sem, c, clk in toks:
            if known[q].get(sem, 0) < c and (sem not in best or best[sem][0] < c):
                best[sem] = (c, clk)
        todo = sorted(best.items(), key=lambda x: -len(x[1][1]))
        for sem, (c, clk) in todo:
            if known[q].get(sem, 0) >= c:
                continue
            if any(s2 != sem and known[q].get(s2, 0) < c2 and k2.get(sem, 0) >= c for s2, (c2, k2) in todo):
                continue
            eng[q].wait_ge(T.sem[sem], c)
            known[q][sem] = c
            for s2, c2 in clk.items():
                if known[q].get(s2, 0) < c2:
                    known[q][s2] = c2

    def op(q, fn, toks, P, sem, inc):
        for b in P:
            toks = toks + [t for q2, t in bank.get(b, {}).items() if q2 != q]
        settle(q, toks)
        ins = fn(eng[q])
        name = sem or "q" + q
        cnt[name] = cnt.get(name, 0) + inc
        ins.then_inc(T.sem[name], inc)
        tok = (name, cnt[name], dict(known[q]))
        for b in P:
            bank.setdefault(b, {})[q] = tok
        return tok

    def send(fn, toks, local, n):
        settle("g", toks)
        fn()
        cnt[local] = n
        return (local, n, dict(known["g"]))

    def lands(sem, n):
        cnt[sem] = n
        return (sem, n, {})

    def finish():
        settle("g", [(s, c, {}) for s, c in cnt.items()])

    return op, send, lands, finish


SHARED = (("Sf", "K2", "dfS", "al"), ("prod1", "df", "dfQ"), ("key2", "kss"), ("o1", "e2p"), ("aqt", "dxs"), ("rg0", "e1", "ksh", "Fp"),
          ("rg1", "sp", "shk", "alY"), ("rg2", "mvS"), ("rg3", "mvQ"), ("stin", "eb"), ("ai", "craw"), ("wi", "cm"), ("pi", "ui"), ("pb", "ua"), ("fx", "FL"), ("aq0", "aq"))
TAKES = {"v": {"V0": 1.75, "y": .25, "W4a": .25, "t12": .25, "RM": .11, "es": .25, "eb": .11, "en": .11, "E": .42, "TT": .42, "sv": .11, "vi": .11, "e2": .11, "FL": .11,
               "Gc": .21, "EC": .21, "fx": .21, "ND": .43, "LT": .053, "D": .053},
         "s": {"Gc": .7, "Gn": .7, "EC": .7, "vx": .25, "TT": .43}, "t": {"rg": .43, "SP": .11, "DT": .11}}
for _k in ("o1", "prod1", "K1", "kss", "cm64", "alY", "Sf", "t64S", "t64Q", "cm", "cu", "K2", "key2", "kept", "shk", "ksh", "ZS", "ZQ", "tb", "mvS", "mvQ", "nS", "nQ", "dfS", "fin",
           "po", "ysw", "so"):
    TAKES["v"][_k] = .2
WAKE = 0.15
REORDER = ("v",)


def _takes(e):
    kind, q, Wr = e[0], e[1], e[4]
    if kind == "send":
        return 0.5
    if kind == "lands":
        return 2.0
    if e[6] is not None:
        return 0.05
    if q == "v" and len(Wr) == 4 and Wr[0].startswith("FL"):
        return 0.7 if "cu" in e[3] else 0.43
    if "plS" in e[3] and Wr[0].startswith("D1"):
        return 0.22
    if "plS" in e[3] and Wr[0].startswith("Gn"):
        return 0.7
    k = Wr[0] if Wr else ""
    tab = TAKES.get(q, {})
    return tab.get(k, tab.get(k.rstrip("0123456789"), .06 if q != "g" else .3))


def _schedule(prog):
    fam = {}
    for f in SHARED:
        for s in f:
            fam[s] = f
    stem = {}

    def st(k):
        if k not in stem:
            stem[k] = k if k in fam else k.rstrip("0123456789")
        return stem[k]

    wr, rd, keys = {}, {}, {}
    deps = []
    for i, e in enumerate(prog):
        d = set()
        for k in e[3]:
            if k in wr:
                d.add(wr[k])
        for k in e[4]:
            if k in wr:
                d.add(wr[k])
            d.update(rd.get(k, ()))
            for s in fam.get(st(k), ()):
                if s != st(k):
                    for k2 in keys.get(s, ()):
                        if k2 in wr:
                            d.add(wr[k2])
                        d.update(rd.get(k2, ()))
        for k in e[3]:
            rd.setdefault(k, []).append(i)
            keys.setdefault(st(k), set()).add(k)
        for k in e[4]:
            wr[k] = i
            rd[k] = []
            keys.setdefault(st(k), set()).add(k)
        d.discard(i)
        deps.append(d)
    n = len(prog)
    cost = [_takes(e) for e in prog]
    nxt = [[] for _ in range(n)]
    for i in range(n):
        for j in deps[i]:
            nxt[j].append(i)
    rank = [0.0] * n
    for i in range(n - 1, -1, -1):
        m = 0.0
        for j in nxt[i]:
            m = max(m, rank[j] + WAKE)
        lat = 5.0 if prog[i][6] is not None else 0.0
        rank[i] = cost[i] + lat + m
    left = [len(d) for d in deps]
    ready = {}
    fifo = {}
    for i, e in enumerate(prog):
        if e[1] not in REORDER and e[1] != "x":
            fifo.setdefault(e[1], []).append(i)
    head = {q: 0 for q in fifo}
    at = [0.0] * n
    free = {}
    for i in range(n):
        if not left[i]:
            ready.setdefault(prog[i][1], set()).add(i)
    order = []
    while len(order) < n:
        pick = None
        for q, r in ready.items():
            c = r
            if q in fifo:
                i = fifo[q][head[q]] if head[q] < len(fifo[q]) else None
                c = (i,) if i in r else ()
            if not c:
                continue
            f = free.get(q, 0.0) if q != "x" else 0.0
            t0 = min(max(f, at[i]) for i in c)
            b = min((-rank[i], i) for i in c if max(f, at[i]) <= t0 + 0.02)[1]
            s = max(f, at[b])
            if pick is None or s < pick[0]:
                pick = (s, b, q)
        s, i, q = pick
        ready[q].discard(i)
        if q in head:
            head[q] += 1
        end = s + cost[i]
        free[q] = end
        order.append((s, i))
        lat = 5.0 if prog[i][6] is not None else 0.0
        for j in nxt[i]:
            at[j] = max(at[j], end + lat + WAKE)
            left[j] -= 1
            if not left[j]:
                ready.setdefault(prog[j][1], set()).add(j)
    return [i for _, i in order], deps


def ks(x, n, a=0):
    return [x + str(k) for k in range(a, n)]


def rank_program(g, core, T, topo):
    rank = T.rank_of(core)
    if rank is None:
        return
    N = len(T.cores)
    op_now, send_now, lands_now, finish = _tracker(g, T)
    prog = []

    def op(q, fn, R=(), Wr=(), P=(), sem=None, inc=1):
        prog.append(("op", q, fn, tuple(R), tuple(Wr), tuple(P), sem, inc))

    def send(fn, R, local, n):
        prog.append(("send", "g", fn, tuple(R), ("@" + local[1:] + "x",), (), None, (local, n)))

    def lands(sem, n, Wr):
        prog.append(("lands", "x", None, ("@" + sem[1:] + "x",), tuple(Wr), (), None, (sem, n)))

    def remote(out, src, there, here, dst):
        rid, pid, _ = topo.addr(dst)
        return lambda: g.remote_dma(out, src, T.sem[there], T.sem[here], pid, rid, topo.mask(core, dst))

    def ts(out, in0, s1, o0, s2=None, o1=None, R=(), Wr=(), P=()):
        if o1 is None:
            op("v", lambda e: e.tensor_scalar(out, in0, s1, None, o0), R, Wr, P)
        else:
            op("v", lambda e: e.tensor_scalar(out, in0, s1, s2, o0, o1), R, Wr, P)

    def tt(out, a, b, o, R=(), Wr=(), P=()):
        op("v", lambda e: e.tensor_tensor(out, a, b, o), R, Wr, P)

    def cp(out, a, R=(), Wr=(), P=()):
        op("v", lambda e: e.tensor_copy(out, a), R, Wr, P)

    def scan(out, a, b, o0, o1, R, Wr, P=()):
        op("v", lambda e: e.tensor_tensor_scan(out, a, b, 0.0, o0, o1), R, Wr, P)

    def fill(x, c, key=None):
        op("v", lambda e: e.memset(x, c), (), [key or x.name])

    def mm(out, l, r, start, stop, R, Wr, P):
        op("t", lambda e: e.matmul(out, l, r, start, stop), R, Wr, P)

    def act(out, a, fn, R, Wr, P=(), **kw):
        op("s", lambda e: e.activation(out, a, fn, **kw), R, Wr, P)

    def iota(out, pattern, base, cmul, key):
        flag = {} if key in ("pi",) else {"allow_small_or_imprecise_dtypes": True}
        op("g", lambda e: e.iota(out, pattern, base, cmul, **flag), (), [key])

    def load(q, k, out, src, Wr):
        op(q, lambda e: e.dma_start(out, src), (), Wr, (), "ld%d" % k, 16)

    def gred(out, src, o, R, Wr, P=()):
        for h in range(8):
            op("v", lambda e, h=h: e.tensor_reduce(out[:, h:h + 1], src[:, h:256:8], AX, o), R, [Wr + str(h)], P)

    load("s", 0, T.craw[:, :], T.act[:, :], ["ai"])
    load("s", 1, T.cm[:, :], T.why[:, :], ["wi"])
    load("s", 2, T.eb[:, :], T.st0[:, :], ["stin"])
    load("s", 3, T.Mdi[:, :], T.bar[:, :], ["bari"])
    for k in range(4):
        load("y", 4 + k, T.E[:, k * 1024:k * 1024 + 1024], T.eff[:, k * 1024:k * 1024 + 1024], ["E%d" % k])
    for k in range(4):
        load("y", 8 + k, T.PT[:, k * 1024:k * 1024 + 1024], T.req[:, k * 1024:k * 1024 + 1024], ["P%d" % k])
    EK = ks("E", 4)

    fill(T.ONE[:, :], 1.0, "ONE")
    op("g", lambda e: e.affine_select(T.ID[:, :], T.ONE[:, :], [[-1, 128]], A.is_equal, 0.0, 0, 1), ["ONE"], ["ID"])
    op("g", lambda e: e.affine_select(T.G8[:, :], T.ONE[:, 0:8], [[-16, 8]], A.is_ge, 0.0, 0, 1), ["ONE"], ["G8"])
    op("g", lambda e: e.affine_select(T.G8[:, :], T.G8[:, :], [[16, 8]], A.is_ge, 0.0, 15, -1), ["G8"], ["G8"])
    iota(T.ui[:, :], [[0, 8]], 0, 1, "pi")
    iota(T.kc[:, :], [[1, 32]], 0, 0, "kc")
    iota(T.KAP[:, :], [[113, 32]], 37, 0, "KAP")
    iota(T.K1c[:, :], [[-1, 32], [0, 8]], 32, 0, "K1c")
    iota(T.K19[:, :], [[-1, 32], [0, 8]], -1, 0, "K19")
    iota(T.K18[:, :], [[-1, 32], [0, 8]], -1, 0, "K18")
    iota(T.K2c[:, :], [[-4096, 32], [0, 8]], 31 * 4096, 0, "K2c")
    iota(T.C32[:, :], [[16, 8]], 0, 0, "C32")
    fill(T.SEL[:, :], 0.0, "SELz")
    fill(T.SEL2[:, :], 0.0, "SEL2z")
    fill(T.D0[:, 0:33 * B:33], -30000.0, "D0i")
    fill(T.Gn[:, W:W + B], 192.0, "Gnx")
    fill(T.ONES32[:, :], 1.0, "ONES32")
    fill(T.SC0[:, :], -1000.0, "SC0z")
    fill(T.SC0[:, 0:128:16], 1000.0, "SC0z")
    fill(T.thr[:, :], 2.0, "thr")

    for k, w in enumerate((-6.0, 2.0, 2.0, -2.0)):
        act(T.IS[:, k * 128:k * 128 + 128], T.ID[:, :], ACT.Copy, ["ID"], ["IS%d" % k], scale=w)
    for k in range(16):
        x = slice(k * 128 + k, k * 128 + 128, 16)
        act(T.SEL[:, x], T.G8[:, :], ACT.Copy, ["G8", "SELz"], ["SEL%d" % k])
        act(T.SEL2[:, x], T.G8[:, :], ACT.Copy, ["G8", "SEL2z"], ["SEL2%d" % k], scale=131072.0)

    cp(T.pl0[:, 0:256], T.craw[:, :], ["ai"], ["plS"])
    ts(T.pl0[:, 256:512], T.cm[:, :], 2, A.add, R=["wi"], Wr=["plQ"])
    ts(T.sq[:, :], T.eb[:, :], 8.0, A.is_ge, -264.0, A.mult, ["stin"], ["sq"])
    tt(T.sc0[:, :], T.eb[:, :], T.sq[:, :], A.add, ["stin", "sq"], ["st"])

    for c in range(8):
        x = slice(c * 512, c * 512 + 512)
        e = "E%d" % (c // 2)
        ts(T.Gc[:, x], T.E[:, x], 4.0, A.is_ge, -520.0, A.mult, [e], ["Gc%d" % c])
        ts(T.EC[:, x], T.E[:, x], 12.0, A.is_ge, 252.0, A.mult, [e], ["EC%d" % c])
        p = T["ps%d" % (c % 4)]
        bk = ["b%d" % (c % 4)]
        pk = ["rg%d" % (c % 4)]
        scan(T.FL[:, x], T.EC[:, x], T.Gc[:, x], A.max, A.add, ["EC%d" % c, "Gc%d" % c], ["fx%d" % c])
        mm(p[:, :], T.ID[:, :], T.E[:, x], True, False, [e, "ID"], pk, bk)
        mm(p[:, :], T.ID[:, :], T.FL[:, x], False, True, ["fx%d" % c], pk, bk)
        act(T.TT[:, x], p[:, :], ACT.Copy, pk, ["TT%d" % c], bk)
    TK = ks("TT", 8)
    ts(T.ua[:, :], T.ui[:, :], 15, A.bitwise_and, R=["pi"], Wr=["pb"])
    tt(T.C32[:, :], T.C32[:, :], T.ua[:, :], A.add, ["C32", "pb"], ["C32"])
    ts(T.Cv[:, :], T.C32[:, :], 33.0, A.mult, 32.0, A.add, ["C32"], ["Cv"])
    ts(T.Cn[:, :], T.C32[:, :], 4096.0, A.add, R=["C32"], Wr=["Cn"])
    ts(T.C32[:, :], T.C32[:, :], 32.0, A.mult, R=["C32", "Cv", "Cn"], Wr=["C32"])
    ts(T.ps5[:, 128:384], T.K1c[:, :], 8192.0, A.mult, R=["K1c"], Wr=["K1c"], P=["b5"])
    cp(T.ps6[:, 256:512], T.K2c[:, :], ["K2c"], ["K2c"], ["b6"])
    fill(T.FOUR[:, :], 4.0, "FOUR")
    for k, w in enumerate((0.5, 248.5, -7.5, -11.5, 5.0)):
        fill(T.SG[:, k:k + 1], w, "sgn")
    ts(T.K19[:, :], T.K19[:, :], 524288.0, A.mult, R=["K19"], Wr=["K19"])
    ts(T.K18[:, :], T.K18[:, :], 262144.0, A.mult, R=["K18"], Wr=["K18"])
    cp(T.barf[:, :], T.Mdi[:, :], ["bari"], ["barf"])
    for k in range(4):
        x = slice(k * 1024, k * 1024 + 1024)
        ts(T.ND[:, x], T.PT[:, x], 12.0, A.is_lt, R=["P%d" % k], Wr=["ND%d" % k])
    NK = ks("ND", 4)
    tt(T.pp[:, 0:64], T.ID[:, 0:64], T.ID[:, 64:128], A.add, ["ID"], ["p1"])
    tt(T.pp[:, 128:160], T.pp[:, 0:32], T.pp[:, 32:64], A.add, ["p1"], ["p2"])
    tt(T.MK16[:, 0:16], T.pp[:, 128:144], T.pp[:, 144:160], A.add, ["p2"], ["MK16"])

    for t in range(VI):
        pl = T["pl%d" % t]
        last = t == VI - 1
        if t:
            n = len(topo.engines(T.cores[(rank - PLAN_GO) % N], core))
            lands("ap%d" % t, n, ["plS"])
            lands("aq%d" % t, n, ["plQ"])
            lands("as%d" % t, len(topo.engines(T.cores[(rank - STATE_GO) % N], core)), ["st"])

        for k in range(32 - NVG):
            act(T.D1[:, k + 1:33 * B:33], T.TT[:, :].indirect(pl[:, k * 8:k * 8 + 8]), ACT.Identity, TK + ["plS"], ["D1%d" % k], bias=12.0 + 4 * k)
        for c in range(8):
            out, src = T.Gn[:, c * 512:c * 512 + 512], T.ND[:, :].indirect(pl[:, c * 32:c * 32 + 32])
            if c < NVD:
                ts(out, src, 188.0, A.mult, 4.0, A.add, NK + ["plS"], ["Gn%d" % c])
            else:
                act(out, src, ACT.Identity, NK + ["plS"], ["Gn%d" % c], scale=188.0, bias=4.0)
        for k in range(32 - NVG, 32):
            ts(T.D1[:, k + 1:33 * B:33], T.TT[:, :].indirect(pl[:, k * 8:k * 8 + 8]), 12.0 + 4 * k, A.add, R=TK + ["plS"], Wr=["D1%d" % k])
        ts(T.D1[:, 0:33 * B:33], T["sc%d" % t][:, :], 4.0, A.add, R=["st"], Wr=["D1i"])
        for k in range(32):
            ts(T.D0[:, k + 1:33 * B:33], T.D1[:, k + 1:33 * B:33], -16.0, A.mult, -4960.0, A.add, ["D1%d" % k], ["D0%d" % k])
        op("v", lambda e: e.tensor_tensor_scan(T.V0[:, :], T.D0[:, :], T.D1[:, :], 0.0, A.min, A.max),
           ks("D0", 32) + ks("D1", 32) + ["D0i", "D1i"], ["V0"])
        if t:
            op("v", lambda e: e.tensor_reduce(T.rs[:, :], T.ps7[:, 280:288], AX, A.add), ["RS"], ["rs"], ["b7"])
            cp(T.ri[:, 0:1], T.rs[:, :], ["rs"], ["ri"])
            ts(T.ri[:, 1:2], T.ri[:, 0:1], 1, A.bitwise_and, R=["ri"], Wr=["rj"])
            ts(T.thr[:, :], T.ri[:, 1:2], 2, A.add, R=["rj"], Wr=["thr"])

        def ndps(c):
            r = c % 4
            mm(T["ps%d" % r][:, :], T.ID[:, :], T.Gn[:, c * 512:c * 512 + 512], True, True, ["ID", "Gn%d" % c], ["rg%d" % r], ["b%d" % r])

        def flaw(c):
            r = c % 4
            for k in range(4 * c, 4 * c + 4):
                tt(T.FL[:, k * 128:k * 128 + 128], T.V0[:, k:33 * B:33], T["ps%d" % r][:, (k % 4) * 128:(k % 4) * 128 + 128], A.is_ge,
                   ["V0", "rg%d" % r], ["FL%d" % k], ["b%d" % r])

        def count(src, key, sel, dst, bk, c, wk):
            for k in range(16):
                mm(dst[:, c * 64:c * 64 + 64], T[sel][:, k * 128:k * 128 + 128], src[:, c * 1024 + k:(c + 1) * 1024:16], k == 0, k == 15,
                   ks(key, 8 * c + 8, 8 * c) + [sel + str(k)], [wk + str(c)] if k in (0, 15) else (), [bk])

        for c in range(4):
            ndps(c)
        flaw(0)
        ndps(4)
        flaw(1)
        ndps(5)
        if EARLY:
            count(T.FL, "FL", "SEL", T.ps4, "b4", 0, "CN")
        flaw(2)
        ndps(6)
        flaw(3)
        ndps(7)
        if not EARLY:
            count(T.FL, "FL", "SEL", T.ps4, "b4", 0, "CN")
        count(T.FL, "FL", "SEL", T.ps4, "b4", 1, "CN")
        for c in (4, 5):
            flaw(c)
        count(T.FL, "FL", "SEL", T.ps4, "b4", 2, "CN")
        for c in (6, 7):
            flaw(c)
        count(T.FL, "FL", "SEL", T.ps4, "b4", 3, "CN")

        v32 = T.V0[:, 32:33 * B:33]
        for k, cut in enumerate((0.5, 248.5, -7.5, -11.5)):
            act(T.pp[:, k * 128:k * 128 + 128], v32, ACT.Sign, ["V0", "sgn"], ["p%d" % (k + 1)], bias=T.SG[:, k:k + 1])
        cp(T.K2[:, :], pl[:, 0:256], ["plS"], ["Sf"])
        act(T.t64S[:, :], T.K2[:, :], ACT.Copy, ["Sf"], ["t64S"], scale=64.0)
        tt(T.ps6[:, 0:256], T.K2[:, :], T.ps5[:, 128:384], A.add, ["Sf", "K1c"], ["K1"], ["b6", "b5"])
        for k in range(5):
            mm(T.ps5[:, 384:512], T.IS[:, (k % 4) * 128:(k % 4) * 128 + 128] if k < 4 else T.ID[:, :], T.pp[:, k * 128:k * 128 + 128] if k < 4 else T.FOUR[:, :],
               k == 0, k == 4, ["IS%d" % (k % 4), "ID", "FOUR", "p%d" % (k % 4 + 1)], ["SP"] if k in (0, 4) else (), ["b5"])
        cp(T.vi[:, :], v32, ["V0"], ["vi"])
        ts(T.e2[:, :], T.vi[:, :], 3, A.bitwise_and, R=["vi"], Wr=["e2"])

        ts(T.o1[:, :], T.ps4[:, 0:256], T.thr[:, :], A.is_ge, R=ks("CN", 4) + ["thr"], Wr=["o1"], P=["b4"])
        tt(T.prod1[:, :], T.o1[:, :], T.ps6[:, 0:256], A.mult, ["o1", "K1"], ["prod1"], ["b6"])
        gred(T.M8i, T.prod1, A.max, ["prod1"], "M8")
        ts(T.xr[:, :], T.M8i[:, :], 13, A.arith_shift_right, R=ks("M8", 8), Wr=["xr"])
        ts(T.sx[:, :], T.M8i[:, :], 4095, A.bitwise_and, R=ks("M8", 8), Wr=["sx"])
        ts(T.xm[:, :], T.M8i[:, :], 6, A.arith_shift_right, 0x7FF80, A.bitwise_and, ks("M8", 8), ["xm"])
        tt(T.oi[:, 0:8], T.Cv[:, :], T.xr[:, :], A.subtract, ["Cv", "xr"], ["oi0"])
        tt(T.oi[:, 8:16], T.Cn[:, :], T.xm[:, :], A.subtract, ["Cn", "xm"], ["oi1"])
        cp(T.ou[:, :], T.oi[:, :], ["oi0", "oi1"], ["ou"])
        GNK = ks("Gn", 8) + ["Gnx"]
        act(T.vx[:, :], T.V0[:, :].indirect(T.ou[:, 0:8]), ACT.Copy, ["V0", "ou"], ["vx"])
        ts(T.t12[:, :], T.V0[:, :].indirect(T.ou[:, 0:8]), 0.0, A.is_ge, 12.0, A.mult, ["V0", "ou"], ["t12"])
        tt(T.y[:, :], T.Gn[:, :].indirect(T.ou[:, 8:16]), T.vx[:, :], A.subtract, GNK + ["ou", "vx"], ["y"])
        mm(T.ps7[:, 0:128], T.y[:, :], T.ID[:, :], True, True, ["y", "ID"], ["DT"], ["b7"])
        tt(T.W4[:, 0:128], T.Gn[:, :].indirect(T.ou[:, 8:16]), T.t12[:, :], A.max, GNK + ["ou", "t12"], ["W4a"])
        op("v", lambda e: e.tensor_tensor_scan(T.RM[:, :], T.SC0[:, :], T.ps7[:, 0:128], 0.0, A.max, A.min), ["SC0z", "DT"], ["RM"], ["b7"])
        ts(T.xf[:, :], T.xr[:, :], -1.0, A.mult, 32.0, A.add, ["xr"], ["xf"])
        for h in range(8):
            out, col = T.LT[:, h * 16:h * 16 + 16], T.RM[:, h * 16 + 15:h * 16 + 16]
            if h < 5:
                ts(out, T.MK16[:, 0:16], col, A.mult, R=["MK16", "RM"], Wr=["LT%d" % h])
            else:
                act(out, T.MK16[:, 0:16], ACT.Identity, ["MK16", "RM"], ["LT%d" % h], scale=col)
        mm(T.ps7[:, 256:264], T.LT[:, :], T.G8[:, :], True, True, ks("LT", 8) + ["G8"], ["D8"], ["b7"])
        for k in range(4):
            mm(T.ps0[:, k * 128:k * 128 + 128], T.ID[:, :], T.W4[:, 0:128], True, True, ["ID", "W4a"], ["rg0"], ["b0"])
        ts(T.ncd[:, :], T.xr[:, :], -8192.0, A.mult, 262144.0, A.add, ["xr"], ["xs"])
        ts(T.di[:, :], T.ps7[:, 256:264], -2048.0, A.mult, -16384.0, A.add, ["D8"], ["di"], ["b7"])
        ts(T.dg[:, :], T.di[:, :], 63 << 13, A.bitwise_and, R=["di"], Wr=["dg"])
        tt(T.d8[:, :], T.dg[:, :], T.ncd[:, :], A.min, ["dg", "xs"], ["d8"])
        cp(T.sxf[:, :], T.sx[:, :], ["sx"], ["sxf"])
        for h in range(8):
            ts(T.prod1[:, h:256:8], T.ps6[:, h:256:8], -262144.0, A.add, T.d8[:, h:h + 1], A.add, ["K1", "d8"], ["df%d" % h], ["b6"])
        for h in range(8):
            op("v", lambda e, h=h: e.tensor_reduce(T.sd[:, h:h + 1], T.prod1[:, h:256:8], AX, A.min, apply_absolute_value=True), ["df%d" % h], ["sd%d" % h])
        SD = ks("sd", 8)
        for k in range(2):
            act(T.base24[:, k * 8:k * 8 + 8], T.xf[:, :], ACT.Copy, ["xf"], ["ba%d" % k])
        act(T.c16[:, 8:16], T.xf[:, :], ACT.Copy, ["xf"], ["c161"])
        act(T.m24[:, 0:8], T.xf[:, :], ACT.Copy, ["xf"], ["m240"], scale=-1.0, bias=99.0)
        act(T.Mb[:, :], T.W4[:, 0:128], ACT.Relu, ["W4a", "sgn"], ["Mb"], scale=-1.0, bias=T.SG[:, 4:5])
        for k in range(1, 4):
            act(T.W4[:, k * 128:k * 128 + 128], T.W4[:, 0:128], ACT.Copy, ["W4a"], ["W4%d" % k])
        tt(T.pr0[:, :], T.sx[:, :], T.sd[:, :], A.mult, ["sx"] + SD, ["pr0"])
        ts(T.bs[:, :], T.pr0[:, :], 5, A.arith_shift_right, R=["pr0"], Wr=["bs"])
        ts(T.bsf[:, :], T.bs[:, :], 97.0 * t, A.add, R=["bs"], Wr=["bsf"])
        for h in range(8):
            ts(T.craw[:, h:256:8], T.KAP[:, :], T.sxf[:, h:h + 1], A.mult, T.bsf[:, h:h + 1], A.add, ["KAP", "sxf", "bsf"], ["craw%d" % h])
        ts(T.cm[:, :], T.craw[:, :], 4095, A.bitwise_and, R=ks("craw", 8), Wr=["cm"])
        cp(T.cu[:, :], T.cm[:, :], ["cm"], ["cu"])

        for c in range(NSC):
            act(T.EC[:, c * 512:c * 512 + 512], T.E[:, :].indirect(T.cu[:, c * 32:c * 32 + 32]), ACT.Copy, EK + ["cu"], ["EC%d" % c])

        def vfuse(c):
            tt(T.FL[:, c * 512:c * 512 + 512], T.E[:, :].indirect(T.cu[:, c * 32:c * 32 + 32]), T.W4[:, :], A.is_ge,
               EK + ["cu", "W4a"] + ks("W4", 4, 1), ks("FL", 4 * c + 4, 4 * c))

        def hit(c):
            tt(T.FL[:, c * 512:c * 512 + 512], T.EC[:, c * 512:c * 512 + 512], T.ps0[:, :], A.is_ge, ["EC%d" % c, "rg0"], ks("FL", 4 * c + 4, 4 * c), ["b0"])

        def score(c):
            count(T.FL, "FL", "SEL2", T.ps4, "b4", c, "CN")

        vfuse(7)
        tt(T.sv[:, :], T.e2[:, :], T.ps5[:, 384:512], A.add, ["e2", "SP"], ["sv"], ["b5"])
        hit(0)
        for k in range(16):
            mm(T.ps7[:, 272:280], T.SEL[:, k * 128:k * 128 + 128], T.sv[:, k:128:16], k == 0, k == 15, ["sv", "SEL%d" % k], ["U8"] if k in (0, 15) else (), ["b7"])
        for k in range(16):
            mm(T.ps5[:, 0:8], T.SEL[:, k * 128:k * 128 + 128], T.Mb[:, k:128:16], k == 0, k == 15, ["Mb", "SEL%d" % k], ["NM"] if k in (0, 15) else (), ["b5"])
        if not last:
            so = T["so%d" % t]
            ts(T.sq[:, :], T.sv[:, :], 8.0, A.is_ge, -264.0, A.mult, ["sv"], ["sq"])
            tt(so[:, :], T.sv[:, :], T.sq[:, :], A.add, ["sv", "sq"], ["so"])
            dst = T.cores[(rank + STATE_GO) % N]
            n = len(topo.engines(core, dst))
            send(remote(T["sc%d" % (t + 1)][:, :], so[:, :], "as%d" % (t + 1), "ls%d" % (t + 1), dst), ["so"], "ls%d" % (t + 1), n)
        hit(1)
        score(0)
        if NSC == 6:
            vfuse(6)
            score(3)
        tt(T.K2[:, :], T.cm[:, :], T.ps6[:, 256:512], A.add, ["K2c", "cm"], ["K2"], ["b6"])
        hit(2)
        if t == 0:
            fill(T.base24[:, 16:24], 0.0, "ba2")
        tt(T.aqt[:, :], T.d8[:, :], T.ncd[:, :], A.subtract, ["d8", "xs"], ["dxs"])
        ts(T.m24[:, 8:16], T.aqt[:, :], 1.0 / 8192, A.mult, R=["dxs"], Wr=["m241"])
        ts(T.cm64[:, :], T.cm[:, :], 64.0, A.mult, -16777216.0, A.add, ["cm"], ["cm64"])
        ts(T.m24[:, 16:24], T.sd[:, :], 64.0, A.mult, 128.0, A.add, SD, ["m242"])
        ts(T.fnd[:, :], T.xr[:, :], 1.0, A.is_ge, 131072.0, A.mult, ["xr"], ["fnd"])
        tt(T.barM[:, :], T.barf[:, :], T.ps5[:, 0:8], A.add, ["barf", "NM"], ["barM"], ["b5"])
        hit(3)
        score(1)
        for k in range(3):
            tt(T.bar24[:, k * 8:k * 8 + 8], T.barM[:, :], T.fnd[:, :], A.mult, ["barM", "fnd"], ["br%d" % k])
        hit(4)
        cp(T.ui[:, :], T.ps7[:, 272:280], ["U8"], ["ui"], ["b7"])
        ts(T.ua[:, :], T.ui[:, :], 31, A.bitwise_and, R=["ui"], Wr=["ua"])
        tt(T.uo[:, :], T.ua[:, :], T.C32[:, :], A.add, ["ua", "C32"], ["uo"])
        cp(T.uu[:, :], T.uo[:, :], ["uo"], ["uu"])
        hit(5)
        score(2)
        ts(T.t64[:, :], pl[:, 256:512], 64.0, A.mult, R=["plQ"], Wr=["t64Q"])
        if NSC == 7:
            hit(6)
            score(3)
        tt(T.es[:, :], T.E[:, :].indirect(T.uu[:, :]), T.sv[:, :], A.add, EK + ["uu", "sv"], ["es"])
        ts(T.en[:, :], T.es[:, :], 1, A.arith_shift_right, R=["es"], Wr=["en"])
        cp(T.eb[:, :], T.en[:, :], ["en"], ["eb"])
        op("v", lambda e: e.tensor_copy(T.E[:, :].indirect(T.uu[:, :]), T.eb[:, :]), ["eb", "uu"], EK)
        if last:
            op("y", lambda e: e.dma_start(T.ye[:, :], T.E[:, :]), EK, ["ye"], (), "ds0", 16)

        tt(T.key2[:, :], T.K2[:, :], T.ps4[:, 0:256], A.add, ["K2"] + ks("CN", 4), ["key2"], ["b4"])
        gred(T.MBi, T.key2, A.max, ["key2"], "MBi")
        MB = ks("MBi", 8)
        for k in range(3):
            tt(T.ret24[:, k * 8:k * 8 + 8], T.MBi[:, :], T.bar24[:, k * 8:k * 8 + 8], A.is_lt, MB + ["br%d" % k], ["ret%d" % k])
        tt(T.pr24[:, :], T.ret24[:, :], T.m24[:, :], A.mult, ks("ret", 3) + ks("m24", 3), ["pr24"])
        ts(T.cb[:, :], T.MBi[:, :], 4095, A.bitwise_and, R=MB, Wr=["cb"])
        ts(T.cbx[:, :], T.cb[:, :], 64.0, A.mult, -16777216.0, A.add, ["cb"], ["cbx"])
        ts(T.nr[:, :], T.ret24[:, 0:8], -1.0, A.mult, 1.0, A.add, ["ret0"], ["nr"])
        tt(T.a24[:, :], T.base24[:, :], T.pr24[:, :], A.add, ["pr24"] + ks("ba", 3), ["a24"])
        for h in range(8):
            ts(T.ps0[:, h:256:8], T.kc[:, :], T.a24[:, h:h + 1], A.min, T.a24[:, 8 + h:9 + h], A.not_equal, ["kc", "a24"], ["e1%d" % h], ["b0"])
            ts(T.o1[:, h:256:8], T.t64[:, h:256:8], T.a24[:, 16 + h:17 + h], A.not_equal, R=["t64Q", "a24"], Wr=["e2p%d" % h])
        tt(T.kept[:, :], T.o1[:, :], T.ps0[:, 0:256], A.min, ks("e1", 8) + ks("e2p", 8), ["kept"], ["b0"])
        if not last:
            cp(T.retb[:, :], T.ret24[:, 0:8], ["ret0"], ["retb"])
            mm(T.ps7[:, 280:288], T.ONE[:, :], T.retb[:, :], True, True, ["ONE", "retb"], ["RS"], ["b7"])
        for h in range(8):
            op("v", lambda e, h=h: e.tensor_tensor_scan(T.ps1[:, h:256:8], T.ONES32[:, :], T.kept[:, h:256:8], 1.0, A.add, A.subtract),
               ["ONES32", "kept"], ["sp%d" % h], ["b1"])
        tt(T.ps1[:, 256:512], T.kept[:, :], T.ps1[:, 0:256], A.mult, ["kept"] + ks("sp", 8), ["shk"], ["b1"])
        op("v", lambda e: e.memset(T.ZS[:, 0:8], 0), (), ["ZS0"])
        op("v", lambda e: e.memset(T.ZQ[:, 0:8], 0), (), ["ZQ0"])
        tt(T.ps0[:, 256:512], T.K19[:, :], T.ps1[:, 256:512], A.add, ["K19", "shk"], ["ksh"], ["b0", "b1"])
        tt(T.key2[:, :], T.K18[:, :], T.ps1[:, 256:512], A.add, ["K18", "shk"], ["kss"], ["b1"])
        tt(T.ZS[:, 8:264], T.t64S[:, :], T.key2[:, :], A.add, ["t64S", "kss"], ["ZS"])
        tt(T.ZQ[:, 8:264], T.t64[:, :], T.ps0[:, 256:512], A.add, ["t64Q", "ksh"], ["ZQ"], ["b0"])
        for k in range(2):
            ts(T.n16[:, k * 8:k * 8 + 8], T.ps1[:, 248:256], -1.0, A.mult, 33.0, A.add, ks("sp", 8), ["n16%d" % k], ["b1"])
        if t == 0:
            fill(T.c16[:, 0:8], 99.0, "c160")
        ts(T.aqt[:, :], T.sd[:, :], 1.0, A.add, R=SD, Wr=["aqt"])
        tt(T.d16[:, :], T.n16[:, :], T.c16[:, :], A.subtract, ["n160", "n161", "c160", "c161"], ["d16"])
        tt(T.cbr[:, :], T.cbx[:, :], T.nr[:, :], A.mult, ["cbx", "nr"], ["cbr"])
        tt(T.aq[:, :], T.aqt[:, :], T.nr[:, :], A.mult, ["aqt", "nr"], ["aq0"])
        tt(T.r16[:, :], T.d16[:, :], T.ret24[:, 0:16], A.mult, ["d16", "ret0", "ret1"], ["r16"])
        ts(T.aq[:, :], T.aq[:, :], 1.0, A.add, R=["aq0"], Wr=["aq"])
        tt(T.f16[:, :], T.r16[:, :], T.c16[:, :], A.add, ["r16", "c160", "c161"], ["f16"])
        for h in range(8):
            act(T.K2[:, h:256:8], T.cm64[:, h:256:8], ACT.Identity, ["cm64", "ret0", "cbr"], ["al%d" % h], scale=T.ret24[:, h:h + 1], bias=T.cbr[:, h:h + 1])
        for h in range(8):
            ts(T.ps0[:, h:256:8], T.kc[:, :], T.f16[:, h:h + 1], A.min, T.f16[:, 8 + h:9 + h], A.is_equal, ["kc", "f16"], ["Fp%d" % h], ["b0"])
        tt(T.ps1[:, 0:256], T.K2[:, :], T.ps0[:, 0:256], A.mult, ks("al", 8) + ks("Fp", 8), ["alY"], ["b0", "b1"])
        for b in range(6):
            s = 1 << b
            m = (33 - s) * 8
            z = ["ZS", "ZS0"]
            q = ["ZQ", "ZQ0"]
            tb = T.tb[:, b * 264:b * 264 + m]
            ts(tb, T.ZS[:, 8 * s:264], b, A.arith_shift_right, 1, A.bitwise_and, z, ["tb%d" % b])
            scan(T.ps2[:, 0:m], tb, T.ZS[:, 8 * s:264], A.max, A.mult, ["tb%d" % b] + z, ["mvS"], ["b2"])
            scan(T.ps3[:, 0:m], tb, T.ZQ[:, 8 * s:264], A.max, A.mult, ["tb%d" % b] + q, ["mvQ"], ["b3"])
            tt(T.ZS[:, 0:m], T.ZS[:, 0:m], T.ps2[:, 0:m], A.min, z + ["mvS"], z, ["b2"])
            tt(T.ZQ[:, 0:m], T.ZQ[:, 0:m], T.ps3[:, 0:m], A.min, q + ["mvQ"], q, ["b3"])
        tt(T.ZS[:, 0:256], T.ZS[:, 0:256], T.ps1[:, 0:256], A.min, z + ["alY"], z, ["b1"])
        ts(T.nS[:, :], T.ZS[:, 0:256], 6, A.arith_shift_right, 4095, A.bitwise_and, ["ZS", "ZS0"], ["nS"])

        def reasons():
            ts(T.nQ[:, :], T.ZQ[:, 0:256], 6, A.arith_shift_right, 8191, A.bitwise_and, ["ZQ", "ZQ0"], ["nQ"])
            for h in range(8):
                ts(T.prod1[:, h:256:8], T.nQ[:, h:256:8], -1.0, A.mult, T.aq[:, h:h + 1], A.add, ["nQ", "aq"], ["dfQ%d" % h])
            tt(T.ps3[:, 0:256], T.prod1[:, :], T.ps0[:, 0:256], A.mult, ks("dfQ", 8) + ks("Fp", 8), ["mvQ"], ["b3", "b0"])

        if not last:
            po = T["plo%d" % t]
            dst = T.cores[(rank + PLAN_GO) % N]
            n = len(topo.engines(core, dst))

            def go(half, s):
                x = slice(half * 256, half * 256 + 256)
                cp(po[:, x], (T.nS, T.nQ)[half][:, :], [("nS", "nQ")[half]], ["po%d" % half])
                send(remote(T["pl%d" % (t + 1)][:, x], po[:, x], "a%s%d" % (s, t + 1), "l%s%d" % (s, t + 1), dst), ["po%d" % half],
                     "l%s%d" % (s, t + 1), n)

            go(0, "p")
            ts(T.pp[:, 0:128], T.eb[:, :], 4.0, A.is_ge, -520.0, A.mult, ["eb"], ["p1"])
            ts(T.pp[:, 128:256], T.eb[:, :], 12.0, A.is_ge, 252.0, A.mult, ["eb"], ["p2"])
            tt(T.pp[:, 256:384], T.pp[:, 0:128], T.pp[:, 128:256], A.add, ["p1", "p2"], ["p3"])
            tt(T.TT[:, :].indirect(T.uu[:, :]), T.eb[:, :], T.pp[:, 256:384], A.add, ["eb", "p3", "uu"], TK)
            reasons()
            tt(T.nQ[:, :], T.nQ[:, :], T.ps3[:, 0:256], A.add, ["nQ", "mvQ"], ["nQ"], ["b3"])
            go(1, "q")
        else:
            cp(T.ysw[:, 0:256], T.nS[:, :], ["nS"], ["ysw0"])
            op("y", lambda e: e.dma_start(T.ys[:, :], T.ysw[:, 0:256]), ["ysw0"], ["ys"], (), "ds1", 16)
            reasons()
            tt(T.K2[:, :], T.nQ[:, :], T.ps3[:, 0:256], A.add, ["nQ", "mvQ"], ["dfS"], ["b3"])
            ts(T.ysw[:, 256:512], T.K2[:, :], 2.0, A.subtract, R=["dfS"], Wr=["ysw1"])
            op("s", lambda e: e.dma_start(T.yw[:, :], T.ysw[:, 256:512]), ["ysw1"], ["yw"], (), "ds2", 16)
    order, deps = _schedule(prog)
    tok = {}
    for i in order:
        kind, q, fn, R, Wr, P, sem, inc = prog[i]
        toks = [tok[j] for j in sorted(deps[i]) if not (q == "t" and prog[j][1] == "t")]
        if kind == "op":
            tok[i] = op_now(q, fn, toks, P, sem, inc)
        elif kind == "send":
            tok[i] = send_now(fn, toks, inc[0], inc[1])
        else:
            tok[i] = lands_now(inc[0], inc[1])
    finish()
